import numpy as np
import ml_dtypes


def mxq(x, axis, fmt="e4m3"):
    dtype, down = {"e4m3": (ml_dtypes.float8_e4m3fn, 7), "e5m2": (ml_dtypes.float8_e5m2, 14)}[fmt]
    v = np.moveaxis(np.asarray(x, np.float32).astype(ml_dtypes.bfloat16).astype(np.float64), axis, -1)
    blocks = v.reshape(v.shape[:-1] + (-1, 32))
    amax = np.abs(blocks).max(-1, keepdims=True)
    byte = np.maximum(np.where(amax > 0, np.frexp(amax)[1] - 1 + 127, 0) - down, 1)
    scale = np.exp2(byte - 127.0)
    codes = (blocks / scale).astype(np.float32).astype(dtype).astype(np.float64)
    return np.moveaxis((codes * scale).reshape(v.shape), -1, axis)


WIDE = False


def mx_kscale(k):
    if not WIDE:
        return np.ones(k)
    levels = np.array([10, -10, 5, -5, 0])
    if k % 512:
        return np.exp2(np.random.permutation(np.resize(levels, k // 32))).repeat(32)
    a = np.empty((k // 512, 16))
    for p in range(k // 512):
        a[p, :8] = np.random.permutation(np.resize(levels, 8))
        for g in range(8):
            far = levels[np.abs(levels - a[p, g]) >= 10]
            a[p, g + 8] = far[np.random.randint(len(far))]
    return np.exp2(a.ravel()).repeat(32)


BF16 = ml_dtypes.bfloat16


def bf(x):
    return np.asarray(x, np.float32).astype(BF16)


def f64(x):
    return np.asarray(x).astype(np.float64)

def planes(Y):
    n, m = Y.shape
    b = f64(bf(Y)).reshape(n // 32, 32, m)
    amax = np.abs(b).max(1)
    byte = np.clip(np.where(amax > 0, np.frexp(amax)[1] - 1 + 127 - 7, 1), 1, 254)
    codes = (b * np.exp2(127.0 - byte)[:, None, :]).reshape(n, m).astype(np.float32).astype(ml_dtypes.float8_e4m3fn).view(np.uint8)
    words = codes.reshape(n // 512, 128, 4, m).transpose(0, 1, 3, 2)
    return np.ascontiguousarray(words), np.ascontiguousarray(byte.astype(np.uint8).reshape(n // 512, 16, m))


H, NQ, NK, DK, DV = 2, 1024, 1024, 512, 512


def scaled_scores(q, k):
    qq = mxq(f64(q), 2, "e4m3")
    kq = mxq(f64(k), 2, "e4m3")
    return (qq @ kq.transpose(0, 2, 1)) / np.sqrt(DK)


def masked_softmax(scores, keep):
    m = np.where(keep, scores, -10000.0)
    e = np.exp(m - m.max(-1, keepdims=True))
    return e / e.sum(-1, keepdims=True)


def setup_inputs():
    s, u = mx_kscale(DK), mx_kscale(DK)
    t = mx_kscale(NK)
    return {
        "q_real": bf(np.random.standard_normal((H, NQ, DK)) * s),
        "k_real": bf(np.random.standard_normal((H, NK, DK)) / s),
        "q_fake": bf(np.random.standard_normal((H, NQ, DK)) * u),
        "k_fake": bf(np.random.standard_normal((H, NK, DK)) / u),
        "v": bf(np.random.standard_normal((H, NK, DV)) / t[:, None]),
        "adj": bf(np.random.standard_normal((NQ, NK))),
        "key_gain": bf(0.5 * np.sqrt(NK) * np.random.standard_normal((H, NK)) * t),
    }


def core(q_real, k_real, q_fake, k_fake, v, adj, key_gain):
    sr = scaled_scores(q_real, k_real)
    sf = scaled_scores(q_fake, k_fake)
    edge = (f64(adj) > 0)[None, :, :]
    pr = masked_softmax(sr, edge)
    pf = masked_softmax(sf, np.logical_not(edge))
    p = pr / 1.5 + pf * (0.5 / 1.5)
    pg = p * f64(key_gain)[:, None, :]
    return mxq(pg, 2, "e4m3") @ mxq(f64(v), 1, "e4m3")


def reference(q_real, k_real, q_fake, k_fake, v, adj, key_gain):
    R_out = core(q_real, k_real, q_fake, k_fake, v, adj, key_gain)
    words, scales = planes(np.moveaxis(R_out, 2, 0).reshape(512, -1))
    return R_out, words, scales

@@ -1,0 +1,420 @@
+from contextlib import ExitStack
+
+import concourse.mybir as mybir
+from concourse.masks import make_identity
+
+H, NQ, NK, DK, DV = 2, 1024, 1024, 512, 512
+FLOPS = 2 * H * NQ * NK * (2 * DK + DV)
+
+F32 = mybir.dt.float32
+BF16 = mybir.dt.bfloat16
+U32 = mybir.dt.uint32
+I32 = mybir.dt.int32
+U8 = mybir.dt.uint8
+FP8X4 = mybir.dt.float8_e4m3fn_x4
+ALU = mybir.AluOpType
+ACT = mybir.ActivationFunctionType
+AX = mybir.AxisListType
+
+P = 128
+SCALE = 1.0 / 512.0 ** 0.5
+MASKED = -10000.0
+KEPT = 2.0 ** 27
+TILES = NQ // P
+UNITS = H * TILES
+
+
+def tile_sanrealfakeedgedualattention_x1_kernel(
+    tc, q_real, k_real, q_fake, k_fake, v, adj, key_gain, out_0, out_1, out_2
+):
+    nc = tc.nc
+    queries = (q_real, q_fake)
+    keys = (k_real, k_fake)
+    words_out = out_1[0].rearrange("p m t -> p (m t)").bitcast(I32)
+    scales_out = out_2[0].bitcast(I32)
+
+    with ExitStack() as ctx:
+        const = ctx.enter_context(tc.tile_pool(name="const", bufs=1))
+        pool = ctx.enter_context(tc.tile_pool(name="work", bufs=2))
+        psum = ctx.enter_context(tc.psum_pool(name="psum", bufs=1))
+        ctx.enter_context(tc.manual_schedule())
+
+        def bank(tag, bufs):
+            b = psum.tile([P, 512], F32, name=tag, tag=tag, bufs=bufs)
+            return b
+
+        ident = const.tile([P, P], F32, name="ident")
+        make_identity(nc, ident[:])
+
+        raws, groups, codes, scales = {}, {}, {}, {}
+
+        def load_chunk(c):
+            kind, br, h, half = c
+            raw = pool.tile([P, 4, DK], BF16, name="raw", tag="raw", bufs=5)
+            src = (queries if kind == "q" else keys)[br][h, 512 * half : 512 * half + 512, :]
+            view = "(t m) k -> m t k" if kind == "q" else "(m t) k -> m t k"
+            nc.sync.dma_start(out=raw[:], in_=src.rearrange(view, t=4))
+            raws[c] = raw
+
+        def turn_chunk(c, part, tag, bufs):
+            raw = raws[c]
+            words = raw[:].rearrange("p t k -> p (t k)").bitcast(F32)
+            b = bank(tag, bufs)
+            for tt in range(2):
+                for u in range(2):
+                    w0 = 256 * (2 * part + tt)
+                    nc.tensor.transpose(
+                        b[:, 128 * (2 * tt + u) : 128 * (2 * tt + u) + 128],
+                        words[:, w0 + u : w0 + 256 : 2],
+                        ident[:],
+                    )
+            return b
+
+        def take_chunk(c, part, b, engine):
+            if part == 0:
+                groups[c] = pool.tile([P, 512, 4], BF16, name="grp", tag="grp", bufs=2, align_bytes=64)
+            dst = groups[c][:].rearrange("p n j -> p (n j)").bitcast(F32)
+            dst = dst[:, 512 * part : 512 * part + 512].rearrange("p (s m u) -> p s m u", s=2, u=2)
+            src = b[:].rearrange("p (s u m) -> p s m u", s=2, u=2)
+            if engine == "v":
+                nc.vector.tensor_copy(out=dst, in_=src)
+            else:
+                nc.scalar.copy(out=dst, in_=src)
+
+        def quant_chunk(c):
+            kind, br, h, half = c
+            key = (kind, br, h)
+            if key not in codes:
+                codes[key] = pool.tile([P, 1024], U32, name="c" + kind + str(br), bufs=2, align_bytes=64)
+                scales[key] = pool.tile([P, 1024], U8, name="s" + kind + str(br), bufs=2, align_bytes=64)
+            nc.vector.quantize_mx(
+                out=codes[key][:, 512 * half : 512 * half + 512].bitcast(FP8X4),
+                scales=scales[key][:, 512 * half : 512 * half + 512],
+                in_=groups[c][:].rearrange("p n j -> p (n j)"),
+            )
+
+        vraw, vcodes, vscales = {}, {}, {}
+
+        def load_v(h, g):
+            r = pool.tile([P, 4, DV], BF16, name="vraw", tag="vraw", bufs=2)
+            nc.sync.dma_start(out=r[:], in_=v[h, 512 * g : 512 * g + 512, :].rearrange("(p j) c -> p j c", j=4))
+            vraw[h, g] = r
+
+        vgrp = {}
+
+        def group_v(h, g):
+            t = pool.tile([P, 512 * 4], BF16, name="vgrp", tag="vgrp", bufs=1, align_bytes=64)
+            nc.gpsimd.tensor_scalar(
+                out=t[:].rearrange("p (t m j) -> p t m j", t=4, j=4),
+                in0=vraw[h, g][:].rearrange("p j (m t) -> p t m j", t=4),
+                scalar1=1.0, scalar2=0.0, op0=ALU.mult, op1=ALU.add,
+            )
+            vgrp[h, g] = t
+
+        def quant_v(h, g):
+            if g == 0:
+                vcodes[h] = const.tile([P, 2, DV], U32, name="vc" + str(h), align_bytes=64)
+                vscales[h] = const.tile([P, 2, DV], U8, name="vs" + str(h), align_bytes=64)
+            nc.vector.quantize_mx(
+                out=vcodes[h][:, g, :].bitcast(FP8X4), scales=vscales[h][:, g, :], in_=vgrp[h, g][:]
+            )
+
+        adjs, bounds = {}, {}
+
+        def load_adj(i):
+            a = pool.tile([P, NK], BF16, name="adj", tag="adj", bufs=2)
+            nc.sync.dma_start(out=a[:], in_=adj[P * i : P * i + P, :])
+            adjs[i] = a
+
+        edges = {}
+
+        def find_edges(i):
+            edge = pool.tile([P, NK], BF16, name="edge", tag="edge", bufs=2)
+            nc.vector.tensor_scalar(out=edge[:], in0=adjs[i][:], scalar1=0.0, scalar2=None, op0=ALU.is_gt)
+            edges[i] = edge
+
+        def make_bounds(i):
+            edge = edges[i]
+            for br in range(2):
+                b = const.tile([P, NK], F32, name="bound" + str(br) + str(i))
+                nc.gpsimd.tensor_scalar(
+                    out=b[:].rearrange("p (g t m) -> p g t m", g=2, t=4),
+                    in0=edge[:].rearrange("p (g m t) -> p g t m", g=2, t=4),
+                    scalar1=(KEPT - MASKED) if br == 0 else (MASKED - KEPT),
+                    scalar2=MASKED if br == 0 else KEPT,
+                    op0=ALU.mult, op1=ALU.add,
+                )
+                bounds[br, i] = b
+
+        gain_raw = const.tile([P, H, 16], BF16, name="gain_raw")
+        gain = const.tile([P, H, 2, 4], F32, name="gain")
+
+        def load_gain():
+            for h in range(H):
+                nc.sync.dma_start(
+                    out=gain_raw[:, h, 0:8].rearrange("p (g t) -> p g t", g=2), in_=key_gain[h].rearrange("(g p t) -> p g t", g=2, t=4)
+                )
+
+        sbank, xs, nms, es, zs, rs, ybank, pgs, pcodes, pscales = ({} for _ in range(10))
+        obank, wbank, outs, pls, plw, plsc = ({} for _ in range(6))
+
+        def scores(n):
+            h, i = divmod(n, TILES)
+            for br in range(2):
+                for g in range(2):
+                    b = bank("s", 3)
+                    nc.tensor.matmul_mx(
+                        out=b[:],
+                        lhsT=codes["q", br, h][:, P * i : P * i + P].bitcast(FP8X4),
+                        lhsT_scale=scales["q", br, h][:, P * i : P * i + P],
+                        rhs=codes["k", br, h][:, 512 * g : 512 * g + 512].bitcast(FP8X4),
+                        rhs_scale=scales["k", br, h][:, 512 * g : 512 * g + 512],
+                        start=True, stop=True,
+                    )
+                    sbank[n, br, g] = b
+
+        def mask(n):
+            h, i = divmod(n, TILES)
+            x = pool.tile([P, 2, NK], F32, name="x", tag="x", bufs=2)
+            xs[n] = x
+            for br in range(2):
+                for g in range(2):
+                    cols = slice(512 * g, 512 * g + 512)
+                    nc.vector.scalar_tensor_tensor(
+                        out=x[:, br, cols], in0=sbank[n, br, g][:], scalar=SCALE,
+                        in1=bounds[br, i][:, cols], op0=ALU.mult, op1=ALU.min,
+                    )
+
+        negs = {}
+
+        def negate(n, br):
+            if br == 0:
+                negs[n] = pool.tile([P, 2, NK], BF16, name="neg", tag="neg", bufs=2)
+            nc.gpsimd.tensor_scalar(
+                out=negs[n][:, br, :], in0=xs[n][:, br, :], scalar1=-1.0, scalar2=0.0,
+                op0=ALU.mult, op1=ALU.add,
+            )
+
+        def rowmax(n):
+            m = pool.tile([P, 2], F32, name="m", tag="m", bufs=3)
+            nms[n] = m
+            for br in range(2):
+                nc.vector.tensor_scalar(
+                    out=negs[n][:, br, :], in0=negs[n][:, br, :], scalar1=1.0, scalar2=None,
+                    op0=ALU.mult, op1=ALU.min, accum_out=m[:, br : br + 1],
+                )
+
+        def exps(n, br):
+            if br == 0:
+                es[n] = pool.tile([P, 2, NK], F32, name="e", tag="e", bufs=3)
+                zs[n] = pool.tile([P, 2], F32, name="z", tag="z", bufs=3)
+            nc.scalar.activation(
+                out=es[n][:, br, :], in_=xs[n][:, br, :], func=ACT.Exp,
+                bias=nms[n][:, br : br + 1], scale=1.0, accum_out=zs[n][:, br : br + 1],
+            )
+
+        def recip(n):
+            r = pool.tile([P, 2], F32, name="r", tag="r", bufs=3)
+            rs[n] = r
+            nc.vector.reciprocal(out=r[:], in_=zs[n][:])
+
+        def norm_real(n):
+            nc.gpsimd.tensor_scalar(
+                out=es[n][:, 0, :], in0=es[n][:, 0, :], scalar1=rs[n][:, 0:1], scalar2=2.0,
+                op0=ALU.mult, op1=ALU.mult,
+            )
+
+        def norm_fake(n):
+            nc.scalar.activation(
+                out=es[n][:, 1, :], in_=es[n][:, 1, :], func=ACT.Copy, scale=rs[n][:, 1:2]
+            )
+
+        def turn_p(n):
+            for g in range(2):
+                b = bank("y", 2)
+                for t in range(4):
+                    col = 512 * g + 128 * t
+                    for br in range(2):
+                        nc.tensor.matmul(
+                            b[:, 128 * t : 128 * t + 128],
+                            lhsT=es[n][:, br, col : col + 128], rhs=ident[:],
+                            start=(br == 0), stop=(br == 1), is_transpose=True,
+                        )
+                ybank[n, g] = b
+
+        def gains(n):
+            h = n // TILES
+            pg = pool.tile([P, 2, P, 4], BF16, name="pg", tag="pg", bufs=3, align_bytes=64)
+            pgs[n] = pg
+            for g in range(2):
+                nc.vector.tensor_tensor(
+                    out=pg[:, g],
+                    in0=ybank[n, g][:].rearrange("p (t m) -> p m t", t=4),
+                    in1=gain[:, h, g, :].unsqueeze(1).to_broadcast([P, P, 4]),
+                    op=ALU.mult,
+                )
+
+        def quant_p(n):
+            pcodes[n] = pool.tile([P, 2, P], U32, name="pc", tag="pc", bufs=3, align_bytes=64)
+            pscales[n] = pool.tile([P, 2, P], U8, name="ps", tag="ps", bufs=3, align_bytes=64)
+            nc.vector.quantize_mx(
+                out=pcodes[n][:].rearrange("p g m -> p (g m)").bitcast(FP8X4),
+                scales=pscales[n][:].rearrange("p g m -> p (g m)"),
+                in_=pgs[n][:].rearrange("p g m t -> p (g m t)"),
+            )
+
+        def pv(n):
+            h = n // TILES
+            b = bank("o", 2)
+            obank[n] = b
+            for g in range(2):
+                nc.tensor.matmul_mx(
+                    out=b[:],
+                    lhsT=pcodes[n][:, g, :].bitcast(FP8X4), lhsT_scale=pscales[n][:, g, :],
+                    rhs=vcodes[h][:, g, :].bitcast(FP8X4), rhs_scale=vscales[h][:, g, :],
+                    start=(g == 0), stop=(g == 1),
+                )
+            b2 = bank("o", 2)
+            wbank[n] = b2
+            for t in range(4):
+                for g in range(2):
+                    cols = slice(128 * t, 128 * t + 128)
+                    nc.tensor.matmul_mx(
+                        out=b2[:, cols],
+                        lhsT=vcodes[h][:, g, cols].bitcast(FP8X4), lhsT_scale=vscales[h][:, g, cols],
+                        rhs=pcodes[n][:, g, :].bitcast(FP8X4), rhs_scale=pscales[n][:, g, :],
+                        start=(g == 0), stop=(g == 1),
+                    )
+
+        def take_out(n):
+            h, i = divmod(n, TILES)
+            o = pool.tile([P, DV], F32, name="o_sb", tag="o_sb", bufs=2)
+            nc.scalar.copy(
+                out=o[:].rearrange("p (m t) -> p m t", t=4),
+                in_=obank[n][:].rearrange("p (t m) -> p m t", t=4),
+            )
+            nc.sync.dma_start(out=out_0[h, P * i : P * i + P, :], in_=o[:])
+            w = pool.tile([P, P, 4], BF16, name="pl", tag="pl", bufs=3, align_bytes=64)
+            pls[n] = w
+            nc.scalar.copy(out=w[:], in_=wbank[n][:].rearrange("p (t m) -> p m t", t=4))
+
+        def quant_out(n):
+            h, i = divmod(n, TILES)
+            if i == 0:
+                plw[h] = const.tile([P, NQ], U32, name="plw" + str(h), align_bytes=64)
+                plsc[h] = const.tile([P, NQ], U8, name="plsc" + str(h), align_bytes=64)
+            cols = slice(P * i, P * i + P)
+            nc.vector.quantize_mx(
+                out=plw[h][:, cols].bitcast(FP8X4), scales=plsc[h][:, cols],
+                in_=pls[n][:].rearrange("p m t -> p (m t)"),
+            )
+            if i % 4 == 3:
+                c0 = P * (i - 3)
+                nc.sync.dma_start(
+                    out=words_out[:, NQ * h + c0 : NQ * h + c0 + 512],
+                    in_=plw[h][:, c0 : c0 + 512].bitcast(I32),
+                )
+            if i == TILES - 1:
+                for big in range(4):
+                    nc.sync.dma_start(
+                        out=scales_out[4 * big : 4 * big + 4, NQ // 4 * h : NQ // 4 * (h + 1)],
+                        in_=plsc[h][32 * big : 32 * big + 4, :].bitcast(I32),
+                    )
+
+        first = [("k", 0, 0, 0), ("k", 0, 0, 1), ("q", 0, 0, 0), ("k", 1, 0, 0), ("k", 1, 0, 1), ("q", 1, 0, 0)]
+        later = {
+            0: [("q", 0, 0, 1)], 1: [("q", 1, 0, 1)],
+            2: [("k", 0, 1, 0)], 3: [("k", 0, 1, 1)], 4: [("k", 1, 1, 0)], 5: [("k", 1, 1, 1)],
+            6: [("q", 0, 1, 0)], 7: [("q", 1, 1, 0)], 8: [("q", 0, 1, 1)], 9: [("q", 1, 1, 1)],
+        }
+        for n, c in enumerate(first):
+            load_chunk(c)
+            if n == 2:
+                load_adj(0)
+        load_gain()
+        load_adj(1)
+        load_v(0, 0)
+        load_v(0, 1)
+        load_adj(2)
+        load_chunk(later[0][0])
+        load_chunk(later[1][0])
+
+        find_edges(0)
+        make_bounds(0)
+        rotation = [("s", 3), ("y", 2), ("o", 2), ("s", 3), ("y", 2), ("o", 2), ("s", 3), ("t", 1)]
+        k = 0
+        for c in first:
+            for part in range(2):
+                tag, bufs = rotation[k % 8]
+                b = turn_chunk(c, part, tag, bufs)
+                take_chunk(c, part, b, "vs"[k % 2])
+                k += 1
+            quant_chunk(c)
+        find_edges(1)
+        make_bounds(1)
+        find_edges(2)
+        nc.vector.tensor_scalar(
+            out=gain[:], in0=gain_raw[:, :, 0:8].rearrange("p h (g t) -> p h g t", g=2), scalar1=1.0 / 3.0, scalar2=None, op0=ALU.mult
+        )
+        scores(0)
+
+        for s in range(UNITS + 4):
+            live = lambda n: 0 <= n < UNITS
+            if s + 2 in later:
+                load_chunk(later[s + 2][0])
+            if s in (3, 4):
+                load_v(1, s - 3)
+            if 0 <= s + 3 < TILES:
+                load_adj(s + 3)
+            chunk = later[s][0] if s in later else None
+            if 0 <= s + 2 < TILES:
+                make_bounds(s + 2)
+            if live(s - 2):
+                turn_p(s - 2)
+            if chunk:
+                ta = turn_chunk(chunk, 0, "t", 1)
+            if live(s - 3):
+                pv(s - 3)
+            if live(s - 1):
+                rowmax(s - 1)
+                exps(s - 1, 0)
+            if live(s):
+                mask(s)
+                negate(s, 0)
+                negate(s, 1)
+            if live(s - 2):
+                gains(s - 2)
+            if chunk:
+                take_chunk(chunk, 0, ta, "s")
+                tb = turn_chunk(chunk, 1, "t", 1)
+            if live(s - 1):
+                exps(s - 1, 1)
+                recip(s - 1)
+            if chunk:
+                take_chunk(chunk, 1, tb, "s")
+            if live(s - 2):
+                quant_p(s - 2)
+            if live(s - 1):
+                norm_real(s - 1)
+            if live(s - 3):
+                take_out(s - 3)
+            if live(s - 1):
+                norm_fake(s - 1)
+            if s == 0:
+                group_v(0, 0)
+                group_v(0, 1)
+            if s == 1:
+                quant_v(0, 0)
+                quant_v(0, 1)
+            if 0 <= s + 3 < TILES:
+                find_edges(s + 3)
+            if s in (6, 7):
+                group_v(1, s - 6)
+            if s in (8, 9):
+                quant_v(1, s - 8)
+            if chunk:
+                quant_chunk(chunk)
+            if live(s - 3):
+                quant_out(s - 3)
+            if live(s + 1):
+                scores(s + 1)

@@ -50,7 +50,7 @@ def tile_sanrealfakeedgedualattention_x1_kernel(
 
         def load_chunk(c):
             kind, br, h, half = c
-            raw = pool.tile([P, 4, DK], BF16, name="raw", tag="raw", bufs=5)
+            raw = pool.tile([P, 4, DK], BF16, name="raw", tag="raw", bufs=6)
             src = (queries if kind == "q" else keys)[br][h, 512 * half : 512 * half + 512, :]
             view = "(t m) k -> m t k" if kind == "q" else "(m t) k -> m t k"
             nc.sync.dma_start(out=raw[:], in_=src.rearrange(view, t=4))
@@ -72,7 +72,7 @@ def tile_sanrealfakeedgedualattention_x1_kernel(
 
         def take_chunk(c, part, b, engine):
             if part == 0:
-                groups[c] = pool.tile([P, 512, 4], BF16, name="grp", tag="grp", bufs=2, align_bytes=64)
+                groups[c] = pool.tile([P, 512, 4], BF16, name="grp", tag="grp", bufs=3, align_bytes=64)
             dst = groups[c][:].rearrange("p n j -> p (n j)").bitcast(F32)
             dst = dst[:, 512 * part : 512 * part + 512].rearrange("p (s m u) -> p s m u", s=2, u=2)
             src = b[:].rearrange("p (s u m) -> p s m u", s=2, u=2)
@@ -96,19 +96,24 @@ def tile_sanrealfakeedgedualattention_x1_kernel(
         vraw, vcodes, vscales = {}, {}, {}
 
         def load_v(h, g):
-            r = pool.tile([P, 4, DV], BF16, name="vraw", tag="vraw", bufs=2)
+            r = pool.tile([P, 4, DV], BF16, name="vraw", tag="raw", bufs=6)
             nc.sync.dma_start(out=r[:], in_=v[h, 512 * g : 512 * g + 512, :].rearrange("(p j) c -> p j c", j=4))
             vraw[h, g] = r
 
         vgrp = {}
 
-        def group_v(h, g):
-            t = pool.tile([P, 512 * 4], BF16, name="vgrp", tag="vgrp", bufs=1, align_bytes=64)
-            nc.gpsimd.tensor_scalar(
-                out=t[:].rearrange("p (t m j) -> p t m j", t=4, j=4),
-                in0=vraw[h, g][:].rearrange("p j (m t) -> p t m j", t=4),
-                scalar1=1.0, scalar2=0.0, op0=ALU.mult, op1=ALU.add,
-            )
+        def group_v(h, g, engine):
+            t = pool.tile([P, 512 * 4], BF16, name="vgrp", tag="vgrp", bufs=2, align_bytes=64)
+            if engine == "s":
+                nc.scalar.copy(
+                    out=t[:].rearrange("p (t m j) -> p t m j", t=4, j=4),
+                    in_=vraw[h, g][:].rearrange("p j (m t) -> p t m j", t=4),
+                )
+            else:
+                nc.vector.tensor_copy(
+                    out=t[:].rearrange("p (t m j) -> p t m j", t=4, j=4),
+                    in_=vraw[h, g][:].rearrange("p j (m t) -> p t m j", t=4),
+                )
             vgrp[h, g] = t
 
         def quant_v(h, g):
@@ -158,9 +163,9 @@ def tile_sanrealfakeedgedualattention_x1_kernel(
         sbank, xs, nms, es, zs, rs, ybank, pgs, pcodes, pscales = ({} for _ in range(10))
         obank, wbank, outs, pls, plw, plsc = ({} for _ in range(6))
 
-        def scores(n):
+        def scores(n, branches=(0, 1)):
             h, i = divmod(n, TILES)
-            for br in range(2):
+            for br in branches:
                 for g in range(2):
                     b = bank("s", 3)
                     nc.tensor.matmul_mx(
@@ -173,11 +178,12 @@ def tile_sanrealfakeedgedualattention_x1_kernel(
                     )
                     sbank[n, br, g] = b
 
-        def mask(n):
+        def mask(n, br):
             h, i = divmod(n, TILES)
-            x = pool.tile([P, 2, NK], F32, name="x", tag="x", bufs=2)
-            xs[n] = x
-            for br in range(2):
+            if br == 0:
+                xs[n] = pool.tile([P, 2, NK], F32, name="x", tag="x", bufs=2)
+            x = xs[n]
+            for br in (br,):
                 for g in range(2):
                     cols = slice(512 * g, 512 * g + 512)
                     nc.vector.scalar_tensor_tensor(
@@ -185,23 +191,23 @@ def tile_sanrealfakeedgedualattention_x1_kernel(
                         in1=bounds[br, i][:, cols], op0=ALU.mult, op1=ALU.min,
                     )
 
-        negs = {}
 
-        def negate(n, br):
-            if br == 0:
-                negs[n] = pool.tile([P, 2, NK], BF16, name="neg", tag="neg", bufs=2)
-            nc.gpsimd.tensor_scalar(
-                out=negs[n][:, br, :], in0=xs[n][:, br, :], scalar1=-1.0, scalar2=0.0,
-                op0=ALU.mult, op1=ALU.add,
-            )
+        halves = {}
 
         def rowmax(n):
             m = pool.tile([P, 2], F32, name="m", tag="m", bufs=3)
             nms[n] = m
+            half = pool.tile([P, 2, 512], BF16, name="half", tag="half", bufs=2)
+            nc.vector.tensor_tensor(
+                out=half[:], in0=xs[n][:, :, 0:512], in1=xs[n][:, :, 512:1024], op=ALU.max
+            )
+            halves[n] = half
+
+        def rowmax2(n):
             for br in range(2):
                 nc.vector.tensor_scalar(
-                    out=negs[n][:, br, :], in0=negs[n][:, br, :], scalar1=1.0, scalar2=None,
-                    op0=ALU.mult, op1=ALU.min, accum_out=m[:, br : br + 1],
+                    out=halves[n][:, br, :], in0=halves[n][:, br, :], scalar1=-1.0, scalar2=None,
+                    op0=ALU.mult, op1=ALU.min, accum_out=nms[n][:, br : br + 1],
                 )
 
         def exps(n, br):
@@ -216,17 +222,20 @@ def tile_sanrealfakeedgedualattention_x1_kernel(
         def recip(n):
             r = pool.tile([P, 2], F32, name="r", tag="r", bufs=3)
             rs[n] = r
+            nc.vector.tensor_scalar(
+                out=zs[n][:, 0:1], in0=zs[n][:, 0:1], scalar1=0.5, scalar2=None, op0=ALU.mult
+            )
             nc.vector.reciprocal(out=r[:], in_=zs[n][:])
 
-        def norm_real(n):
-            nc.gpsimd.tensor_scalar(
-                out=es[n][:, 0, :], in0=es[n][:, 0, :], scalar1=rs[n][:, 0:1], scalar2=2.0,
-                op0=ALU.mult, op1=ALU.mult,
-            )
-
-        def norm_fake(n):
+        def norm(n, br):
+            if n >= UNITS - 2:
+                nc.vector.tensor_scalar(
+                    out=es[n][:, br, :], in0=es[n][:, br, :], scalar1=rs[n][:, br : br + 1],
+                    scalar2=None, op0=ALU.mult,
+                )
+                return
             nc.scalar.activation(
-                out=es[n][:, 1, :], in_=es[n][:, 1, :], func=ACT.Copy, scale=rs[n][:, 1:2]
+                out=es[n][:, br, :], in_=es[n][:, br, :], func=ACT.Copy, scale=rs[n][:, br : br + 1]
             )
 
         def turn_p(n):
@@ -242,11 +251,12 @@ def tile_sanrealfakeedgedualattention_x1_kernel(
                         )
                 ybank[n, g] = b
 
-        def gains(n):
+        def gains(n, g):
             h = n // TILES
-            pg = pool.tile([P, 2, P, 4], BF16, name="pg", tag="pg", bufs=3, align_bytes=64)
-            pgs[n] = pg
-            for g in range(2):
+            if g == 0:
+                pgs[n] = pool.tile([P, 2, P, 4], BF16, name="pg", tag="pg", bufs=3, align_bytes=64)
+            pg = pgs[n]
+            for g in (g,):
                 nc.vector.tensor_tensor(
                     out=pg[:, g],
                     in0=ybank[n, g][:].rearrange("p (t m) -> p m t", t=4),
@@ -294,6 +304,8 @@ def tile_sanrealfakeedgedualattention_x1_kernel(
                 in_=obank[n][:].rearrange("p (t m) -> p m t", t=4),
             )
             nc.sync.dma_start(out=out_0[h, P * i : P * i + P, :], in_=o[:])
+
+        def take_planes(n):
             w = pool.tile([P, P, 4], BF16, name="pl", tag="pl", bufs=3, align_bytes=64)
             pls[n] = w
             nc.scalar.copy(out=w[:], in_=wbank[n][:].rearrange("p (t m) -> p m t", t=4))
@@ -323,9 +335,9 @@ def tile_sanrealfakeedgedualattention_x1_kernel(
 
         first = [("k", 0, 0, 0), ("k", 0, 0, 1), ("q", 0, 0, 0), ("k", 1, 0, 0), ("k", 1, 0, 1), ("q", 1, 0, 0)]
         later = {
-            0: [("q", 0, 0, 1)], 1: [("q", 1, 0, 1)],
-            2: [("k", 0, 1, 0)], 3: [("k", 0, 1, 1)], 4: [("k", 1, 1, 0)], 5: [("k", 1, 1, 1)],
-            6: [("q", 0, 1, 0)], 7: [("q", 1, 1, 0)], 8: [("q", 0, 1, 1)], 9: [("q", 1, 1, 1)],
+            0: [("q", 0, 0, 1), ("q", 1, 0, 1)], 1: [("k", 0, 1, 0)], 2: [("k", 0, 1, 1)],
+            3: [("k", 1, 1, 0)], 4: [("k", 1, 1, 1)], 5: [("q", 0, 1, 0)], 6: [("q", 1, 1, 0)],
+            8: [("q", 0, 1, 1)], 9: [("q", 1, 1, 1)],
         }
         for n, c in enumerate(first):
             load_chunk(c)
@@ -337,84 +349,99 @@ def tile_sanrealfakeedgedualattention_x1_kernel(
         load_v(0, 1)
         load_adj(2)
         load_chunk(later[0][0])
+        load_chunk(later[0][1])
         load_chunk(later[1][0])
 
-        find_edges(0)
-        make_bounds(0)
         rotation = [("s", 3), ("y", 2), ("o", 2), ("s", 3), ("y", 2), ("o", 2), ("s", 3), ("t", 1)]
         k = 0
         for c in first:
             for part in range(2):
                 tag, bufs = rotation[k % 8]
                 b = turn_chunk(c, part, tag, bufs)
-                take_chunk(c, part, b, "vs"[k % 2])
+                take_chunk(c, part, b, "ssvssvsssvsv"[k])
                 k += 1
+            if c == first[1]:
+                find_edges(0)
+                make_bounds(0)
             quant_chunk(c)
+            if c == first[2]:
+                scores(0, (0,))
+                mask(0, 0)
+        scores(0, (1,))
+        mask(0, 1)
         find_edges(1)
         make_bounds(1)
         find_edges(2)
         nc.vector.tensor_scalar(
             out=gain[:], in0=gain_raw[:, :, 0:8].rearrange("p h (g t) -> p h g t", g=2), scalar1=1.0 / 3.0, scalar2=None, op0=ALU.mult
         )
-        scores(0)
 
-        for s in range(UNITS + 4):
+        ta = turn_chunk(later[0][0], 0, "t", 1)
+        for s in range(UNITS + 7):
             live = lambda n: 0 <= n < UNITS
-            if s + 2 in later:
-                load_chunk(later[s + 2][0])
+            chunks = later.get(s, [])
+            for c in later.get(s + 2, []):
+                load_chunk(c)
             if s in (3, 4):
                 load_v(1, s - 3)
             if 0 <= s + 3 < TILES:
                 load_adj(s + 3)
-            chunk = later[s][0] if s in later else None
             if 0 <= s + 2 < TILES:
                 make_bounds(s + 2)
-            if live(s - 2):
-                turn_p(s - 2)
-            if chunk:
-                ta = turn_chunk(chunk, 0, "t", 1)
             if live(s - 3):
-                pv(s - 3)
+                turn_p(s - 3)
+            if live(s - 4):
+                pv(s - 4)
+            if live(s) and s:
+                mask(s, 0)
             if live(s - 1):
-                rowmax(s - 1)
                 exps(s - 1, 0)
-            if live(s):
-                mask(s)
-                negate(s, 0)
-                negate(s, 1)
-            if live(s - 2):
-                gains(s - 2)
-            if chunk:
-                take_chunk(chunk, 0, ta, "s")
-                tb = turn_chunk(chunk, 1, "t", 1)
+            if chunks:
+                take_chunk(chunks[0], 0, ta, "s")
+                tb = turn_chunk(chunks[0], 1, "t", 1)
             if live(s - 1):
                 exps(s - 1, 1)
-                recip(s - 1)
-            if chunk:
-                take_chunk(chunk, 1, tb, "s")
+            if live(s - 5):
+                take_out(s - 5)
+                take_planes(s - 5)
             if live(s - 2):
-                quant_p(s - 2)
-            if live(s - 1):
-                norm_real(s - 1)
+                recip(s - 2)
+                norm(s - 2, 0)
+            if chunks:
+                take_chunk(chunks[0], 1, tb, "s")
+            if live(s - 2):
+                norm(s - 2, 1)
+            if live(s) and s:
+                mask(s, 1)
             if live(s - 3):
-                take_out(s - 3)
-            if live(s - 1):
-                norm_fake(s - 1)
+                gains(s - 3, 0)
+            if live(s):
+                rowmax(s)
+            if live(s - 3):
+                gains(s - 3, 1)
+            if live(s):
+                rowmax2(s)
+            if live(s - 3):
+                quant_p(s - 3)
             if s == 0:
-                group_v(0, 0)
-                group_v(0, 1)
-            if s == 1:
-                quant_v(0, 0)
-                quant_v(0, 1)
-            if 0 <= s + 3 < TILES:
-                find_edges(s + 3)
-            if s in (6, 7):
-                group_v(1, s - 6)
+                group_v(0, 0, "s")
+                group_v(0, 1, "s")
+            for c in later.get(s - 1, []):
+                quant_chunk(c)
+            if live(s - 6):
+                quant_out(s - 6)
+            if s in (2, 3):
+                quant_v(0, s - 2)
             if s in (8, 9):
                 quant_v(1, s - 8)
-            if chunk:
-                quant_chunk(chunk)
-            if live(s - 3):
-                quant_out(s - 3)
+            if s in (7, 8):
+                group_v(1, s - 7, "v")
+            if 0 <= s + 3 < TILES:
+                find_edges(s + 3)
+            for c in chunks[1:]:
+                for part in range(2):
+                    take_chunk(c, part, turn_chunk(c, part, "t", 1), "s")
+            if s + 1 in later:
+                ta = turn_chunk(later[s + 1][0], 0, "t", 1)
             if live(s + 1):
                 scores(s + 1)

@@ -14,12 +14,12 @@ U8 = mybir.dt.uint8
 FP8X4 = mybir.dt.float8_e4m3fn_x4
 ALU = mybir.AluOpType
 ACT = mybir.ActivationFunctionType
-AX = mybir.AxisListType
 
 P = 128
 SCALE = 1.0 / 512.0 ** 0.5
 MASKED = -10000.0
-KEPT = 2.0 ** 27
+EPS = 2.0 ** -14
+BOUND = -MASKED / SCALE / EPS
 TILES = NQ // P
 UNITS = H * TILES
 
@@ -39,8 +39,10 @@ def tile_sanrealfakeedgedualattention_x1_kernel(
         psum = ctx.enter_context(tc.psum_pool(name="psum", bufs=1))
         ctx.enter_context(tc.manual_schedule())
 
-        def bank(tag, bufs):
-            b = psum.tile([P, 512], F32, name=tag, tag=tag, bufs=bufs)
+        BANKS = {"s": 3, "y": 2, "o": 2, "t": 1}
+
+        def bank(tag):
+            b = psum.tile([P, 512], F32, name=tag, tag=tag, bufs=BANKS[tag])
             return b
 
         ident = const.tile([P, P], F32, name="ident")
@@ -48,18 +50,17 @@ def tile_sanrealfakeedgedualattention_x1_kernel(
 
         raws, groups, codes, scales = {}, {}, {}, {}
 
-        def load_chunk(c):
+        def load_chunk(c, t0=0, t1=4):
             kind, br, h, half = c
-            raw = pool.tile([P, 4, DK], BF16, name="raw", tag="raw", bufs=6)
+            if c not in raws:
+                raws[c] = pool.tile([P, 4, DK], BF16, name="raw", tag="raw", bufs=10)
             src = (queries if kind == "q" else keys)[br][h, 512 * half : 512 * half + 512, :]
             view = "(t m) k -> m t k" if kind == "q" else "(m t) k -> m t k"
-            nc.sync.dma_start(out=raw[:], in_=src.rearrange(view, t=4))
-            raws[c] = raw
+            nc.sync.dma_start(out=raws[c][:, t0:t1, :], in_=src.rearrange(view, t=4)[:, t0:t1, :])
 
-        def turn_chunk(c, part, tag, bufs):
-            raw = raws[c]
-            words = raw[:].rearrange("p t k -> p (t k)").bitcast(F32)
-            b = bank(tag, bufs)
+        def turn_chunk(c, part, tag):
+            words = raws[c][:].rearrange("p t k -> p (t k)").bitcast(F32)
+            b = bank(tag)
             for tt in range(2):
                 for u in range(2):
                     w0 = 256 * (2 * part + tt)
@@ -71,49 +72,43 @@ def tile_sanrealfakeedgedualattention_x1_kernel(
             return b
 
         def take_chunk(c, part, b, engine):
-            if part == 0:
-                groups[c] = pool.tile([P, 512, 4], BF16, name="grp", tag="grp", bufs=3, align_bytes=64)
-            dst = groups[c][:].rearrange("p n j -> p (n j)").bitcast(F32)
-            dst = dst[:, 512 * part : 512 * part + 512].rearrange("p (s m u) -> p s m u", s=2, u=2)
+            grp = pool.tile([P, 256, 4], BF16, name="grp", tag="grp", bufs=4, align_bytes=64)
+            groups[c, part] = grp
+            dst = grp[:].rearrange("p n j -> p (n j)").bitcast(F32).rearrange("p (s m u) -> p s m u", s=2, u=2)
             src = b[:].rearrange("p (s u m) -> p s m u", s=2, u=2)
             if engine == "v":
                 nc.vector.tensor_copy(out=dst, in_=src)
             else:
                 nc.scalar.copy(out=dst, in_=src)
 
-        def quant_chunk(c):
+        def quant_chunk(c, part):
             kind, br, h, half = c
             key = (kind, br, h)
             if key not in codes:
                 codes[key] = pool.tile([P, 1024], U32, name="c" + kind + str(br), bufs=2, align_bytes=64)
                 scales[key] = pool.tile([P, 1024], U8, name="s" + kind + str(br), bufs=2, align_bytes=64)
+            c0 = 512 * half + 256 * part
             nc.vector.quantize_mx(
-                out=codes[key][:, 512 * half : 512 * half + 512].bitcast(FP8X4),
-                scales=scales[key][:, 512 * half : 512 * half + 512],
-                in_=groups[c][:].rearrange("p n j -> p (n j)"),
+                out=codes[key][:, c0 : c0 + 256].bitcast(FP8X4),
+                scales=scales[key][:, c0 : c0 + 256],
+                in_=groups[c, part][:].rearrange("p n j -> p (n j)"),
             )
 
-        vraw, vcodes, vscales = {}, {}, {}
+        vraw, vcodes, vscales, vgrp = {}, {}, {}, {}
 
         def load_v(h, g):
-            r = pool.tile([P, 4, DV], BF16, name="vraw", tag="raw", bufs=6)
+            r = pool.tile([P, 4, DV], BF16, name="vraw", tag="raw", bufs=10)
             nc.sync.dma_start(out=r[:], in_=v[h, 512 * g : 512 * g + 512, :].rearrange("(p j) c -> p j c", j=4))
             vraw[h, g] = r
 
-        vgrp = {}
-
         def group_v(h, g, engine):
             t = pool.tile([P, 512 * 4], BF16, name="vgrp", tag="vgrp", bufs=2, align_bytes=64)
+            dst = t[:].rearrange("p (t m j) -> p t m j", t=4, j=4)
+            src = vraw[h, g][:].rearrange("p j (m t) -> p t m j", t=4)
             if engine == "s":
-                nc.scalar.copy(
-                    out=t[:].rearrange("p (t m j) -> p t m j", t=4, j=4),
-                    in_=vraw[h, g][:].rearrange("p j (m t) -> p t m j", t=4),
-                )
+                nc.scalar.copy(out=dst, in_=src)
             else:
-                nc.vector.tensor_copy(
-                    out=t[:].rearrange("p (t m j) -> p t m j", t=4, j=4),
-                    in_=vraw[h, g][:].rearrange("p j (m t) -> p t m j", t=4),
-                )
+                nc.vector.tensor_copy(out=dst, in_=src)
             vgrp[h, g] = t
 
         def quant_v(h, g):
@@ -127,27 +122,15 @@ def tile_sanrealfakeedgedualattention_x1_kernel(
         adjs, bounds = {}, {}
 
         def load_adj(i):
-            a = pool.tile([P, NK], BF16, name="adj", tag="adj", bufs=2)
+            a = const.tile([P, NK], BF16, name="adj" + str(i))
             nc.sync.dma_start(out=a[:], in_=adj[P * i : P * i + P, :])
             adjs[i] = a
 
-        edges = {}
-
-        def find_edges(i):
-            edge = pool.tile([P, NK], BF16, name="edge", tag="edge", bufs=2)
-            nc.vector.tensor_scalar(out=edge[:], in0=adjs[i][:], scalar1=0.0, scalar2=None, op0=ALU.is_gt)
-            edges[i] = edge
-
         def make_bounds(i):
-            edge = edges[i]
-            for br in range(2):
-                b = const.tile([P, NK], F32, name="bound" + str(br) + str(i))
-                nc.gpsimd.tensor_scalar(
-                    out=b[:].rearrange("p (g t m) -> p g t m", g=2, t=4),
-                    in0=edge[:].rearrange("p (g m t) -> p g t m", g=2, t=4),
-                    scalar1=(KEPT - MASKED) if br == 0 else (MASKED - KEPT),
-                    scalar2=MASKED if br == 0 else KEPT,
-                    op0=ALU.mult, op1=ALU.add,
+            for br, op in enumerate((ALU.is_gt, ALU.is_le)):
+                b = const.tile([P, NK], BF16, name="bound" + str(br) + str(i))
+                nc.vector.tensor_scalar(
+                    out=b[:], in0=adjs[i][:], scalar1=0.0, scalar2=EPS, op0=op, op1=ALU.subtract
                 )
                 bounds[br, i] = b
 
@@ -157,116 +140,132 @@ def tile_sanrealfakeedgedualattention_x1_kernel(
         def load_gain():
             for h in range(H):
                 nc.sync.dma_start(
-                    out=gain_raw[:, h, 0:8].rearrange("p (g t) -> p g t", g=2), in_=key_gain[h].rearrange("(g p t) -> p g t", g=2, t=4)
+                    out=gain_raw[:, h, 0:8].rearrange("p (g t) -> p g t", g=2),
+                    in_=key_gain[h].rearrange("(g p t) -> p g t", g=2, t=4),
                 )
 
-        sbank, xs, nms, es, zs, rs, ybank, pgs, pcodes, pscales = ({} for _ in range(10))
-        obank, wbank, outs, pls, plw, plsc = ({} for _ in range(6))
-
-        def scores(n, branches=(0, 1)):
-            h, i = divmod(n, TILES)
-            for br in branches:
-                for g in range(2):
-                    b = bank("s", 3)
-                    nc.tensor.matmul_mx(
-                        out=b[:],
-                        lhsT=codes["q", br, h][:, P * i : P * i + P].bitcast(FP8X4),
-                        lhsT_scale=scales["q", br, h][:, P * i : P * i + P],
-                        rhs=codes["k", br, h][:, 512 * g : 512 * g + 512].bitcast(FP8X4),
-                        rhs_scale=scales["k", br, h][:, 512 * g : 512 * g + 512],
-                        start=True, stop=True,
-                    )
-                    sbank[n, br, g] = b
-
-        def mask(n, br):
-            h, i = divmod(n, TILES)
-            if br == 0:
-                xs[n] = pool.tile([P, 2, NK], F32, name="x", tag="x", bufs=2)
-            x = xs[n]
-            for br in (br,):
-                for g in range(2):
-                    cols = slice(512 * g, 512 * g + 512)
-                    nc.vector.scalar_tensor_tensor(
-                        out=x[:, br, cols], in0=sbank[n, br, g][:], scalar=SCALE,
-                        in1=bounds[br, i][:, cols], op0=ALU.mult, op1=ALU.min,
-                    )
-
-
-        halves = {}
-
-        def rowmax(n):
-            m = pool.tile([P, 2], F32, name="m", tag="m", bufs=3)
-            nms[n] = m
-            half = pool.tile([P, 2, 512], BF16, name="half", tag="half", bufs=2)
-            nc.vector.tensor_tensor(
-                out=half[:], in0=xs[n][:, :, 0:512], in1=xs[n][:, :, 512:1024], op=ALU.max
+        def scale_gain():
+            nc.vector.tensor_scalar(
+                out=gain[:], in0=gain_raw[:, :, 0:8].rearrange("p h (g t) -> p h g t", g=2),
+                scalar1=1.0 / 3.0, scalar2=None, op0=ALU.mult,
             )
-            halves[n] = half
 
-        def rowmax2(n):
-            for br in range(2):
-                nc.vector.tensor_scalar(
-                    out=halves[n][:, br, :], in0=halves[n][:, br, :], scalar1=-1.0, scalar2=None,
-                    op0=ALU.mult, op1=ALU.min, accum_out=nms[n][:, br : br + 1],
+        sbank, xs, nms, halves, es, zs, rs, diags, ybank, pgs, pcodes, pscales = ({} for _ in range(12))
+        obank, wbank, pls, plw, plsc = ({} for _ in range(5))
+
+        def scores(n, parts):
+            h, i = divmod(n, TILES)
+            for br, g in parts:
+                b = bank("s")
+                nc.tensor.matmul_mx(
+                    out=b[:],
+                    lhsT=codes["q", br, h][:, P * i : P * i + P].bitcast(FP8X4),
+                    lhsT_scale=scales["q", br, h][:, P * i : P * i + P],
+                    rhs=codes["k", br, h][:, 512 * g : 512 * g + 512].bitcast(FP8X4),
+                    rhs_scale=scales["k", br, h][:, 512 * g : 512 * g + 512],
+                    start=True, stop=True,
                 )
+                sbank[n, br, g] = b
+
+        def mask(n, parts):
+            i = n % TILES
+            if n not in xs:
+                xs[n] = pool.tile([P, 2, NK], F32, name="x", tag="x", bufs=2)
+            for br, g in parts:
+                cols = slice(512 * g, 512 * g + 512)
+                nc.vector.scalar_tensor_tensor(
+                    out=xs[n][:, br, cols].rearrange("p (t m) -> p t m", t=4),
+                    in0=bounds[br, i][:, cols].rearrange("p (m t) -> p t m", t=4), scalar=BOUND,
+                    in1=sbank[n, br, g][:].rearrange("p (t m) -> p t m", t=4), op0=ALU.mult, op1=ALU.min,
+                )
+
+        def halve(n, br):
+            if br == 0:
+                nms[n] = pool.tile([P, 2], F32, name="m", tag="m", bufs=3)
+                halves[n] = pool.tile([P, 2, 512], BF16, name="half", tag="half", bufs=2)
+            nc.vector.tensor_tensor(
+                out=halves[n][:, br, :], in0=xs[n][:, br, 0:512], in1=xs[n][:, br, 512:1024], op=ALU.max
+            )
+
+        def negmax(n, br):
+            nc.vector.tensor_scalar(
+                out=halves[n][:, br, :], in0=halves[n][:, br, :], scalar1=-SCALE, scalar2=None,
+                op0=ALU.mult, op1=ALU.min, accum_out=nms[n][:, br : br + 1],
+            )
 
         def exps(n, br):
             if br == 0:
-                es[n] = pool.tile([P, 2, NK], F32, name="e", tag="e", bufs=3)
+                es[n] = pool.tile([P, 2, NK], F32, name="e", tag="e", bufs=2)
                 zs[n] = pool.tile([P, 2], F32, name="z", tag="z", bufs=3)
             nc.scalar.activation(
                 out=es[n][:, br, :], in_=xs[n][:, br, :], func=ACT.Exp,
-                bias=nms[n][:, br : br + 1], scale=1.0, accum_out=zs[n][:, br : br + 1],
+                bias=nms[n][:, br : br + 1], scale=SCALE, accum_out=zs[n][:, br : br + 1],
             )
 
-        def recip(n):
-            r = pool.tile([P, 2], F32, name="r", tag="r", bufs=3)
-            rs[n] = r
+        def pe_norm(n, g):
+            return n < UNITS - 2 and g == 0
+
+        def halve_z(n):
             nc.vector.tensor_scalar(
                 out=zs[n][:, 0:1], in0=zs[n][:, 0:1], scalar1=0.5, scalar2=None, op0=ALU.mult
             )
-            nc.vector.reciprocal(out=r[:], in_=zs[n][:])
 
-        def norm(n, br):
+        def recip(n):
+            rs[n] = pool.tile([P, 2], F32, name="r", tag="r", bufs=3)
+            nc.vector.reciprocal(out=rs[n][:], in_=zs[n][:])
+
+        def diag(n):
+            if pe_norm(n, 0):
+                diags[n] = pool.tile([P, P], F32, name="diag", tag="diag", bufs=3)
+                nc.vector.tensor_scalar(
+                    out=diags[n][:], in0=ident[:], scalar1=rs[n][:, 0:1], scalar2=None, op0=ALU.mult
+                )
+
+        def norm(n):
+            cut = 512 if pe_norm(n, 0) else 0
+            real = es[n][:, 0, cut:NK]
+            fake = es[n][:, 1, :]
             if n >= UNITS - 2:
                 nc.vector.tensor_scalar(
-                    out=es[n][:, br, :], in0=es[n][:, br, :], scalar1=rs[n][:, br : br + 1],
-                    scalar2=None, op0=ALU.mult,
+                    out=real, in0=real, scalar1=rs[n][:, 0:1], scalar2=None, op0=ALU.mult
                 )
-                return
-            nc.scalar.activation(
-                out=es[n][:, br, :], in_=es[n][:, br, :], func=ACT.Copy, scale=rs[n][:, br : br + 1]
-            )
+            else:
+                nc.scalar.activation(out=real, in_=real, func=ACT.Copy, scale=rs[n][:, 0:1])
+            nc.scalar.activation(out=fake, in_=fake, func=ACT.Copy, scale=rs[n][:, 1:2])
 
-        def turn_p(n):
-            for g in range(2):
-                b = bank("y", 2)
-                for t in range(4):
-                    col = 512 * g + 128 * t
-                    for br in range(2):
-                        nc.tensor.matmul(
-                            b[:, 128 * t : 128 * t + 128],
-                            lhsT=es[n][:, br, col : col + 128], rhs=ident[:],
-                            start=(br == 0), stop=(br == 1), is_transpose=True,
-                        )
-                ybank[n, g] = b
+        def turn_p(n, g):
+            b = bank("y")
+            for t in range(4):
+                col = 512 * g + 128 * t
+                out = b[:, 128 * t : 128 * t + 128]
+                if pe_norm(n, g):
+                    nc.tensor.matmul(
+                        out, lhsT=es[n][:, 0, col : col + 128], rhs=diags[n][:], start=True, stop=False
+                    )
+                else:
+                    nc.tensor.matmul(
+                        out, lhsT=es[n][:, 0, col : col + 128], rhs=ident[:],
+                        start=True, stop=False, is_transpose=True,
+                    )
+                nc.tensor.matmul(
+                    out, lhsT=es[n][:, 1, col : col + 128], rhs=ident[:],
+                    start=False, stop=True, is_transpose=True,
+                )
+            ybank[n, g] = b
 
         def gains(n, g):
-            h = n // TILES
             if g == 0:
-                pgs[n] = pool.tile([P, 2, P, 4], BF16, name="pg", tag="pg", bufs=3, align_bytes=64)
-            pg = pgs[n]
-            for g in (g,):
-                nc.vector.tensor_tensor(
-                    out=pg[:, g],
-                    in0=ybank[n, g][:].rearrange("p (t m) -> p m t", t=4),
-                    in1=gain[:, h, g, :].unsqueeze(1).to_broadcast([P, P, 4]),
-                    op=ALU.mult,
-                )
+                pgs[n] = pool.tile([P, 2, P, 4], BF16, name="pg", tag="pg", bufs=2, align_bytes=64)
+            nc.vector.tensor_tensor(
+                out=pgs[n][:, g],
+                in0=ybank[n, g][:].rearrange("p (t m) -> p m t", t=4),
+                in1=gain[:, n // TILES, g, :].unsqueeze(1).to_broadcast([P, P, 4]),
+                op=ALU.mult,
+            )
 
         def quant_p(n):
-            pcodes[n] = pool.tile([P, 2, P], U32, name="pc", tag="pc", bufs=3, align_bytes=64)
-            pscales[n] = pool.tile([P, 2, P], U8, name="ps", tag="ps", bufs=3, align_bytes=64)
+            pcodes[n] = pool.tile([P, 2, P], U32, name="pc", tag="pc", bufs=2, align_bytes=64)
+            pscales[n] = pool.tile([P, 2, P], U8, name="ps", tag="ps", bufs=2, align_bytes=64)
             nc.vector.quantize_mx(
                 out=pcodes[n][:].rearrange("p g m -> p (g m)").bitcast(FP8X4),
                 scales=pscales[n][:].rearrange("p g m -> p (g m)"),
@@ -275,22 +274,20 @@ def tile_sanrealfakeedgedualattention_x1_kernel(
 
         def pv(n):
             h = n // TILES
-            b = bank("o", 2)
-            obank[n] = b
+            obank[n] = bank("o")
             for g in range(2):
                 nc.tensor.matmul_mx(
-                    out=b[:],
+                    out=obank[n][:],
                     lhsT=pcodes[n][:, g, :].bitcast(FP8X4), lhsT_scale=pscales[n][:, g, :],
                     rhs=vcodes[h][:, g, :].bitcast(FP8X4), rhs_scale=vscales[h][:, g, :],
                     start=(g == 0), stop=(g == 1),
                 )
-            b2 = bank("o", 2)
-            wbank[n] = b2
+            wbank[n] = bank("o")
             for t in range(4):
+                cols = slice(128 * t, 128 * t + 128)
                 for g in range(2):
-                    cols = slice(128 * t, 128 * t + 128)
                     nc.tensor.matmul_mx(
-                        out=b2[:, cols],
+                        out=wbank[n][:, cols],
                         lhsT=vcodes[h][:, g, cols].bitcast(FP8X4), lhsT_scale=vscales[h][:, g, cols],
                         rhs=pcodes[n][:, g, :].bitcast(FP8X4), rhs_scale=pscales[n][:, g, :],
                         start=(g == 0), stop=(g == 1),
@@ -304,11 +301,8 @@ def tile_sanrealfakeedgedualattention_x1_kernel(
                 in_=obank[n][:].rearrange("p (t m) -> p m t", t=4),
             )
             nc.sync.dma_start(out=out_0[h, P * i : P * i + P, :], in_=o[:])
-
-        def take_planes(n):
-            w = pool.tile([P, P, 4], BF16, name="pl", tag="pl", bufs=3, align_bytes=64)
-            pls[n] = w
-            nc.scalar.copy(out=w[:], in_=wbank[n][:].rearrange("p (t m) -> p m t", t=4))
+            pls[n] = pool.tile([P, P, 4], BF16, name="pl", tag="pl", bufs=3, align_bytes=64)
+            nc.scalar.copy(out=pls[n][:], in_=wbank[n][:].rearrange("p (t m) -> p m t", t=4))
 
         def quant_out(n):
             h, i = divmod(n, TILES)
@@ -333,115 +327,120 @@ def tile_sanrealfakeedgedualattention_x1_kernel(
                         in_=plsc[h][32 * big : 32 * big + 4, :].bitcast(I32),
                     )
 
-        first = [("k", 0, 0, 0), ("k", 0, 0, 1), ("q", 0, 0, 0), ("k", 1, 0, 0), ("k", 1, 0, 1), ("q", 1, 0, 0)]
-        later = {
-            0: [("q", 0, 0, 1), ("q", 1, 0, 1)], 1: [("k", 0, 1, 0)], 2: [("k", 0, 1, 1)],
-            3: [("k", 1, 1, 0)], 4: [("k", 1, 1, 1)], 5: [("q", 0, 1, 0)], 6: [("q", 1, 1, 0)],
-            8: [("q", 0, 1, 1)], 9: [("q", 1, 1, 1)],
-        }
-        for n, c in enumerate(first):
-            load_chunk(c)
-            if n == 2:
-                load_adj(0)
-        load_gain()
+        def later(s):
+            if s == 0:
+                return [(("q", 0, 0, 0), 1), (("q", 1, 0, 0), 1)]
+            if s in (1, 2):
+                return [(("q", s - 1, 0, 1), 0), (("q", s - 1, 0, 1), 1)]
+            if 3 <= s <= 6:
+                c = ("k", (s - 3) // 2, 1, (s - 3) % 2)
+                return [(c, 0), (c, 1)]
+            if s in (7, 8):
+                return [(("q", 0, 1, 0), s - 7), (("q", 1, 1, 0), s - 7)]
+            if s in (9, 10):
+                return [(("q", s - 9, 1, 1), 0), (("q", s - 9, 1, 1), 1)]
+            return []
+
+        load_chunk(("q", 0, 0, 0), 0, 2)
+        load_chunk(("k", 0, 0, 0))
+        load_adj(0)
+        load_chunk(("k", 0, 0, 1))
+        load_chunk(("q", 1, 0, 0), 0, 2)
+        load_chunk(("k", 1, 0, 0))
+        load_chunk(("k", 1, 0, 1))
         load_adj(1)
-        load_v(0, 0)
-        load_v(0, 1)
+        load_chunk(("q", 0, 0, 0), 2, 4)
+        load_chunk(("q", 1, 0, 0), 2, 4)
         load_adj(2)
-        load_chunk(later[0][0])
-        load_chunk(later[0][1])
-        load_chunk(later[1][0])
+        load_gain()
+        load_v(0, 0)
+        load_chunk(("q", 0, 0, 1))
+        load_adj(3)
+        load_v(0, 1)
+        load_chunk(("q", 1, 0, 1))
+        for i in range(4, TILES):
+            load_adj(i)
 
-        rotation = [("s", 3), ("y", 2), ("o", 2), ("s", 3), ("y", 2), ("o", 2), ("s", 3), ("t", 1)]
-        k = 0
-        for c in first:
-            for part in range(2):
-                tag, bufs = rotation[k % 8]
-                b = turn_chunk(c, part, tag, bufs)
-                take_chunk(c, part, b, "ssvssvsssvsv"[k])
-                k += 1
-            if c == first[1]:
-                find_edges(0)
+        first = [(("q", 0, 0, 0), 0), (("k", 0, 0, 0), 0), (("k", 0, 0, 0), 1), (("k", 0, 0, 1), 0), (("k", 0, 0, 1), 1),
+                 (("q", 1, 0, 0), 0), (("k", 1, 0, 0), 0), (("k", 1, 0, 0), 1), (("k", 1, 0, 1), 0), (("k", 1, 0, 1), 1)]
+        rotation = "sssyyootyo"
+        for k, (c, part) in enumerate(first):
+            take_chunk(c, part, turn_chunk(c, part, rotation[k]), "svsvsvsvsv"[k])
+            if k == 1:
                 make_bounds(0)
-            quant_chunk(c)
-            if c == first[2]:
-                scores(0, (0,))
-                mask(0, 0)
-        scores(0, (1,))
-        mask(0, 1)
-        find_edges(1)
+            quant_chunk(c, part)
+        scores(0, ((0, 0), (0, 1), (1, 0)))
+        ta = turn_chunk(*later(0)[0], "t")
         make_bounds(1)
-        find_edges(2)
-        nc.vector.tensor_scalar(
-            out=gain[:], in0=gain_raw[:, :, 0:8].rearrange("p h (g t) -> p h g t", g=2), scalar1=1.0 / 3.0, scalar2=None, op0=ALU.mult
-        )
 
-        ta = turn_chunk(later[0][0], 0, "t", 1)
-        for s in range(UNITS + 7):
+        for s in range(UNITS + 5):
             live = lambda n: 0 <= n < UNITS
-            chunks = later.get(s, [])
-            for c in later.get(s + 2, []):
-                load_chunk(c)
+            banks = later(s)
+            if s >= 1:
+                for c, part in later(s + 2):
+                    if part == 0 and c not in raws:
+                        load_chunk(c)
             if s in (3, 4):
                 load_v(1, s - 3)
-            if 0 <= s + 3 < TILES:
-                load_adj(s + 3)
-            if 0 <= s + 2 < TILES:
+            if 2 <= s + 2 < TILES:
                 make_bounds(s + 2)
             if live(s - 3):
-                turn_p(s - 3)
+                gains(s - 3, 0)
+                gains(s - 3, 1)
+            if live(s - 2):
+                turn_p(s - 2, 0)
+            if live(s):
+                mask(s, ((0, 0), (0, 1)))
+                scores(s, ((1, 1),))
             if live(s - 4):
-                pv(s - 4)
-            if live(s) and s:
-                mask(s, 0)
+                take_out(s - 4)
             if live(s - 1):
                 exps(s - 1, 0)
-            if chunks:
-                take_chunk(chunks[0], 0, ta, "s")
-                tb = turn_chunk(chunks[0], 1, "t", 1)
+            if banks:
+                take_chunk(*banks[0], ta, "s")
+                tb = turn_chunk(*banks[1], "t")
+            if live(s - 2):
+                turn_p(s - 2, 1)
             if live(s - 1):
                 exps(s - 1, 1)
-            if live(s - 5):
-                take_out(s - 5)
-                take_planes(s - 5)
-            if live(s - 2):
-                recip(s - 2)
-                norm(s - 2, 0)
-            if chunks:
-                take_chunk(chunks[0], 1, tb, "s")
-            if live(s - 2):
-                norm(s - 2, 1)
-            if live(s) and s:
-                mask(s, 1)
-            if live(s - 3):
-                gains(s - 3, 0)
+            if banks:
+                take_chunk(*banks[1], tb, "s")
             if live(s):
-                rowmax(s)
-            if live(s - 3):
-                gains(s - 3, 1)
-            if live(s):
-                rowmax2(s)
+                mask(s, ((1, 0),))
+                halve(s, 0)
             if live(s - 3):
                 quant_p(s - 3)
+            if live(s - 3):
+                pv(s - 3)
+            if live(s):
+                mask(s, ((1, 1),))
+                negmax(s, 0)
+            if live(s - 1):
+                halve_z(s - 1)
+            if live(s):
+                halve(s, 1)
+            if live(s - 1):
+                recip(s - 1)
+            for c, part in banks:
+                quant_chunk(c, part)
+            if live(s - 1):
+                diag(s - 1)
+                norm(s - 1)
+            if s in (0, 1):
+                group_v(0, s, "s")
+            if live(s - 4):
+                quant_out(s - 4)
             if s == 0:
-                group_v(0, 0, "s")
-                group_v(0, 1, "s")
-            for c in later.get(s - 1, []):
-                quant_chunk(c)
-            if live(s - 6):
-                quant_out(s - 6)
-            if s in (2, 3):
-                quant_v(0, s - 2)
+                scale_gain()
+            if s in (1, 2):
+                quant_v(0, s - 1)
             if s in (8, 9):
                 quant_v(1, s - 8)
             if s in (7, 8):
                 group_v(1, s - 7, "v")
-            if 0 <= s + 3 < TILES:
-                find_edges(s + 3)
-            for c in chunks[1:]:
-                for part in range(2):
-                    take_chunk(c, part, turn_chunk(c, part, "t", 1), "s")
-            if s + 1 in later:
-                ta = turn_chunk(later[s + 1][0], 0, "t", 1)
+            if live(s):
+                negmax(s, 1)
+            if later(s + 1):
+                ta = turn_chunk(*later(s + 1)[0], "t")
             if live(s + 1):
-                scores(s + 1)
+                scores(s + 1, ((0, 0), (0, 1), (1, 0)))

@@ -15,6 +15,11 @@ FP8X4 = mybir.dt.float8_e4m3fn_x4
 ALU = mybir.AluOpType
 ACT = mybir.ActivationFunctionType
 
+GCONV = ()
+PEG = (0,)
+GV1 = "s"
+BODY = (("po",-4,),("bd",2,),("z0",-2,),("pp",-4,),("m00",0,),("s11",0,),("s10",0,),("ca",0,),("m01",0,),("g0",-3,),("e0",-1,),("ld",0,),("a0",-2,),("to",-4,),("h0",0,),("tb",0,),("vq",0,),("qa",-1,),("m11",0,),("g1",-3,),("m10",0,),("rc",-1,),("h1",0,),("xc",-2,),("qb",-1,),("qo",-5,),("a1",-2,),("vg",0,),("db",-1,),("qp",-3,),("tp",-4,),("s01",1,),("cb",0,),("n1",0,),("xq",-3,),("n0",0,),("s00",1,),("z1",-1,),("dg",-1,),("e1",0,),("ta",1,),("xt",0,),)
+
 P = 128
 SCALE = 1.0 / 512.0 ** 0.5
 MASKED = -10000.0
@@ -72,7 +77,7 @@ def tile_sanrealfakeedgedualattention_x1_kernel(
             return b
 
         def take_chunk(c, part, b, engine):
-            grp = pool.tile([P, 256, 4], BF16, name="grp", tag="grp", bufs=4, align_bytes=64)
+            grp = pool.tile([P, 256, 4], BF16, name="grp", tag="grp", bufs=6, align_bytes=64)
             groups[c, part] = grp
             dst = grp[:].rearrange("p n j -> p (n j)").bitcast(F32).rearrange("p (s m u) -> p s m u", s=2, u=2)
             src = b[:].rearrange("p (s u m) -> p s m u", s=2, u=2)
@@ -180,21 +185,28 @@ def tile_sanrealfakeedgedualattention_x1_kernel(
                 )
 
         def halve(n, br):
-            if br == 0:
+            if n not in nms:
                 nms[n] = pool.tile([P, 2], F32, name="m", tag="m", bufs=3)
-                halves[n] = pool.tile([P, 2, 512], BF16, name="half", tag="half", bufs=2)
-            nc.vector.tensor_tensor(
-                out=halves[n][:, br, :], in0=xs[n][:, br, 0:512], in1=xs[n][:, br, 512:1024], op=ALU.max
-            )
+            if br in GCONV:
+                halves[n, br] = pool.tile([P, NK], BF16, name="neg" + str(br), bufs=2)
+                nc.gpsimd.tensor_scalar(
+                    out=halves[n, br][:], in0=xs[n][:, br, :], scalar1=-SCALE, scalar2=0.0,
+                    op0=ALU.mult, op1=ALU.add,
+                )
+            else:
+                halves[n, br] = pool.tile([P, 512], BF16, name="half" + str(br), bufs=2)
+                nc.vector.tensor_tensor(
+                    out=halves[n, br][:], in0=xs[n][:, br, 0:512], in1=xs[n][:, br, 512:1024], op=ALU.max
+                )
 
         def negmax(n, br):
             nc.vector.tensor_scalar(
-                out=halves[n][:, br, :], in0=halves[n][:, br, :], scalar1=-SCALE, scalar2=None,
+                out=halves[n, br][:], in0=halves[n, br][:], scalar1=1.0 if br in GCONV else -SCALE, scalar2=None,
                 op0=ALU.mult, op1=ALU.min, accum_out=nms[n][:, br : br + 1],
             )
 
         def exps(n, br):
-            if br == 0:
+            if n not in es:
                 es[n] = pool.tile([P, 2, NK], F32, name="e", tag="e", bufs=2)
                 zs[n] = pool.tile([P, 2], F32, name="z", tag="z", bufs=3)
             nc.scalar.activation(
@@ -203,11 +215,11 @@ def tile_sanrealfakeedgedualattention_x1_kernel(
             )
 
         def pe_norm(n, g):
-            return n < UNITS - 2 and g == 0
+            return n < UNITS - 2 and g in PEG
 
-        def halve_z(n):
+        def double(n):
             nc.vector.tensor_scalar(
-                out=zs[n][:, 0:1], in0=zs[n][:, 0:1], scalar1=0.5, scalar2=None, op0=ALU.mult
+                out=rs[n][:, 0:1], in0=rs[n][:, 0:1], scalar1=2.0, scalar2=None, op0=ALU.mult
             )
 
         def recip(n):
@@ -217,44 +229,43 @@ def tile_sanrealfakeedgedualattention_x1_kernel(
         def diag(n):
             if pe_norm(n, 0):
                 diags[n] = pool.tile([P, P], F32, name="diag", tag="diag", bufs=3)
-                nc.vector.tensor_scalar(
-                    out=diags[n][:], in0=ident[:], scalar1=rs[n][:, 0:1], scalar2=None, op0=ALU.mult
+                nc.gpsimd.tensor_scalar(
+                    out=diags[n][:], in0=ident[:], scalar1=rs[n][:, 0:1], scalar2=0.0, op0=ALU.mult, op1=ALU.add
                 )
 
-        def norm(n):
+        def norm(n, br):
             cut = 512 if pe_norm(n, 0) else 0
             real = es[n][:, 0, cut:NK]
             fake = es[n][:, 1, :]
-            if n >= UNITS - 2:
+            if br and n == UNITS - 1:
+                nc.vector.tensor_scalar(
+                    out=fake[:, 512:NK], in0=fake[:, 512:NK], scalar1=rs[n][:, 1:2], scalar2=None, op0=ALU.mult
+                )
+                nc.scalar.activation(out=fake[:, 0:512], in_=fake[:, 0:512], func=ACT.Copy, scale=rs[n][:, 1:2])
+            elif br:
+                nc.scalar.activation(out=fake, in_=fake, func=ACT.Copy, scale=rs[n][:, 1:2])
+            elif n >= UNITS - 2:
                 nc.vector.tensor_scalar(
                     out=real, in0=real, scalar1=rs[n][:, 0:1], scalar2=None, op0=ALU.mult
                 )
             else:
                 nc.scalar.activation(out=real, in_=real, func=ACT.Copy, scale=rs[n][:, 0:1])
-            nc.scalar.activation(out=fake, in_=fake, func=ACT.Copy, scale=rs[n][:, 1:2])
 
         def turn_p(n, g):
             b = bank("y")
             for t in range(4):
                 col = 512 * g + 128 * t
                 out = b[:, 128 * t : 128 * t + 128]
-                if pe_norm(n, g):
+                for k, br in enumerate((t % 2, 1 - t % 2)):
+                    by_diag = br == 0 and pe_norm(n, g)
                     nc.tensor.matmul(
-                        out, lhsT=es[n][:, 0, col : col + 128], rhs=diags[n][:], start=True, stop=False
+                        out, lhsT=es[n][:, br, col : col + 128], rhs=(diags[n] if by_diag else ident)[:],
+                        start=(k == 0), stop=(k == 1), is_transpose=not by_diag,
                     )
-                else:
-                    nc.tensor.matmul(
-                        out, lhsT=es[n][:, 0, col : col + 128], rhs=ident[:],
-                        start=True, stop=False, is_transpose=True,
-                    )
-                nc.tensor.matmul(
-                    out, lhsT=es[n][:, 1, col : col + 128], rhs=ident[:],
-                    start=False, stop=True, is_transpose=True,
-                )
             ybank[n, g] = b
 
         def gains(n, g):
-            if g == 0:
+            if n not in pgs:
                 pgs[n] = pool.tile([P, 2, P, 4], BF16, name="pg", tag="pg", bufs=2, align_bytes=64)
             nc.vector.tensor_tensor(
                 out=pgs[n][:, g],
@@ -282,6 +293,9 @@ def tile_sanrealfakeedgedualattention_x1_kernel(
                     rhs=vcodes[h][:, g, :].bitcast(FP8X4), rhs_scale=vscales[h][:, g, :],
                     start=(g == 0), stop=(g == 1),
                 )
+
+        def pvp(n):
+            h = n // TILES
             wbank[n] = bank("o")
             for t in range(4):
                 cols = slice(128 * t, 128 * t + 128)
@@ -301,8 +315,11 @@ def tile_sanrealfakeedgedualattention_x1_kernel(
                 in_=obank[n][:].rearrange("p (t m) -> p m t", t=4),
             )
             nc.sync.dma_start(out=out_0[h, P * i : P * i + P, :], in_=o[:])
+
+        def take_pl(n):
             pls[n] = pool.tile([P, P, 4], BF16, name="pl", tag="pl", bufs=3, align_bytes=64)
-            nc.scalar.copy(out=pls[n][:], in_=wbank[n][:].rearrange("p (t m) -> p m t", t=4))
+            copy = nc.vector.tensor_copy if n >= UNITS - 2 else nc.scalar.copy
+            copy(out=pls[n][:], in_=wbank[n][:].rearrange("p (t m) -> p m t", t=4))
 
         def quant_out(n):
             h, i = divmod(n, TILES)
@@ -314,11 +331,11 @@ def tile_sanrealfakeedgedualattention_x1_kernel(
                 out=plw[h][:, cols].bitcast(FP8X4), scales=plsc[h][:, cols],
                 in_=pls[n][:].rearrange("p m t -> p (m t)"),
             )
-            if i % 4 == 3:
-                c0 = P * (i - 3)
+            done = {3: (0, 4), 6: (4, 7), 7: (7, 8)}.get(i)
+            if done:
+                c0, c1 = P * done[0], P * done[1]
                 nc.sync.dma_start(
-                    out=words_out[:, NQ * h + c0 : NQ * h + c0 + 512],
-                    in_=plw[h][:, c0 : c0 + 512].bitcast(I32),
+                    out=words_out[:, NQ * h + c0 : NQ * h + c1], in_=plw[h][:, c0:c1].bitcast(I32)
                 )
             if i == TILES - 1:
                 for big in range(4):
@@ -327,19 +344,19 @@ def tile_sanrealfakeedgedualattention_x1_kernel(
                         in_=plsc[h][32 * big : 32 * big + 4, :].bitcast(I32),
                     )
 
+        def both(half, h, part):
+            return [(("q", 0, h, half), part), (("q", 1, h, half), part)]
+
+        def whole(br, half):
+            return [(("k", br, 1, half), 0), (("k", br, 1, half), 1)]
+
+        prep = {
+            0: both(0, 0, 1) + whole(0, 0), 1: whole(0, 1), 2: both(1, 0, 0), 3: whole(1, 0), 4: both(1, 0, 1),
+            5: whole(1, 1), 6: both(0, 1, 0), 7: both(0, 1, 1), 9: both(1, 1, 0), 11: both(1, 1, 1),
+        }
+
         def later(s):
-            if s == 0:
-                return [(("q", 0, 0, 0), 1), (("q", 1, 0, 0), 1)]
-            if s in (1, 2):
-                return [(("q", s - 1, 0, 1), 0), (("q", s - 1, 0, 1), 1)]
-            if 3 <= s <= 6:
-                c = ("k", (s - 3) // 2, 1, (s - 3) % 2)
-                return [(c, 0), (c, 1)]
-            if s in (7, 8):
-                return [(("q", 0, 1, 0), s - 7), (("q", 1, 1, 0), s - 7)]
-            if s in (9, 10):
-                return [(("q", s - 9, 1, 1), 0), (("q", s - 9, 1, 1), 1)]
-            return []
+            return prep.get(s, [])
 
         load_chunk(("q", 0, 0, 0), 0, 2)
         load_chunk(("k", 0, 0, 0))
@@ -347,16 +364,18 @@ def tile_sanrealfakeedgedualattention_x1_kernel(
         load_chunk(("k", 0, 0, 1))
         load_chunk(("q", 1, 0, 0), 0, 2)
         load_chunk(("k", 1, 0, 0))
-        load_chunk(("k", 1, 0, 1))
         load_adj(1)
+        load_chunk(("k", 1, 0, 1))
+        load_adj(2)
+        load_v(0, 0)
         load_chunk(("q", 0, 0, 0), 2, 4)
         load_chunk(("q", 1, 0, 0), 2, 4)
-        load_adj(2)
         load_gain()
-        load_v(0, 0)
-        load_chunk(("q", 0, 0, 1))
+        load_chunk(("k", 0, 1, 0))
         load_adj(3)
         load_v(0, 1)
+        load_chunk(("k", 0, 1, 1))
+        load_chunk(("q", 0, 0, 1))
         load_chunk(("q", 1, 0, 1))
         for i in range(4, TILES):
             load_adj(i)
@@ -365,82 +384,88 @@ def tile_sanrealfakeedgedualattention_x1_kernel(
                  (("q", 1, 0, 0), 0), (("k", 1, 0, 0), 0), (("k", 1, 0, 0), 1), (("k", 1, 0, 1), 0), (("k", 1, 0, 1), 1)]
         rotation = "sssyyootyo"
         for k, (c, part) in enumerate(first):
-            take_chunk(c, part, turn_chunk(c, part, rotation[k]), "svsvsvsvsv"[k])
-            if k == 1:
-                make_bounds(0)
+            take_chunk(c, part, turn_chunk(c, part, rotation[k]), "ssssssssss"[k])
+            if k in (1, 7, 9):
+                make_bounds((1, 7, 9).index(k))
             quant_chunk(c, part)
         scores(0, ((0, 0), (0, 1), (1, 0)))
-        ta = turn_chunk(*later(0)[0], "t")
-        make_bounds(1)
+        turned0 = turn_chunk(*later(0)[0], "t")
+        group_v(0, 0, "s")
 
-        for s in range(UNITS + 5):
-            live = lambda n: 0 <= n < UNITS
-            banks = later(s)
-            if s >= 1:
+        first_step = {"ta": -1}
+        turned = {(0, 0): turned0}
+
+        def chunk_turn(s, k):
+            if s in prep:
+                turned[s, k] = turn_chunk(*prep[s][k], "t")
+
+        def chunk_take(s, k):
+            if s in prep:
+                take_chunk(*prep[s][k], turned[s, k], "s")
+
+        def chunk_quant(s, k):
+            if s in prep:
+                quant_chunk(*prep[s][k])
+
+        def extra(s, what):
+            if s == 0:
+                for k, item in enumerate(prep[0][2:]):
+                    if what == 0:
+                        turned[0, 2 + k] = turn_chunk(*item, "o")
+                    elif what == 1:
+                        take_chunk(*item, turned[0, 2 + k], "s")
+                    else:
+                        quant_chunk(*item)
+
+        def loads(s):
+            if s >= 0:
                 for c, part in later(s + 2):
-                    if part == 0 and c not in raws:
+                    if c not in raws:
                         load_chunk(c)
-            if s in (3, 4):
-                load_v(1, s - 3)
-            if 2 <= s + 2 < TILES:
-                make_bounds(s + 2)
-            if live(s - 3):
-                gains(s - 3, 0)
-                gains(s - 3, 1)
-            if live(s - 2):
-                turn_p(s - 2, 0)
-            if live(s):
-                mask(s, ((0, 0), (0, 1)))
-                scores(s, ((1, 1),))
-            if live(s - 4):
-                take_out(s - 4)
-            if live(s - 1):
-                exps(s - 1, 0)
-            if banks:
-                take_chunk(*banks[0], ta, "s")
-                tb = turn_chunk(*banks[1], "t")
-            if live(s - 2):
-                turn_p(s - 2, 1)
-            if live(s - 1):
-                exps(s - 1, 1)
-            if banks:
-                take_chunk(*banks[1], tb, "s")
-            if live(s):
-                mask(s, ((1, 0),))
-                halve(s, 0)
-            if live(s - 3):
-                quant_p(s - 3)
-            if live(s - 3):
-                pv(s - 3)
-            if live(s):
-                mask(s, ((1, 1),))
-                negmax(s, 0)
-            if live(s - 1):
-                halve_z(s - 1)
-            if live(s):
-                halve(s, 1)
-            if live(s - 1):
-                recip(s - 1)
-            for c, part in banks:
-                quant_chunk(c, part)
-            if live(s - 1):
-                diag(s - 1)
-                norm(s - 1)
-            if s in (0, 1):
-                group_v(0, s, "s")
-            if live(s - 4):
-                quant_out(s - 4)
+                if s in (3, 4):
+                    load_v(1, s - 3)
+
+        def make_b(i):
+            if 3 <= i < TILES:
+                make_bounds(i)
+
+        def v_group(s):
+            if s == 1:
+                group_v(0, 1, "s")
+            if s in (7, 8):
+                group_v(1, s - 7, GV1)
+
+        def v_quant(s):
             if s == 0:
                 scale_gain()
             if s in (1, 2):
                 quant_v(0, s - 1)
             if s in (8, 9):
                 quant_v(1, s - 8)
-            if s in (7, 8):
-                group_v(1, s - 7, "v")
-            if live(s):
-                negmax(s, 1)
-            if later(s + 1):
-                ta = turn_chunk(*later(s + 1)[0], "t")
-            if live(s + 1):
-                scores(s + 1, ((0, 0), (0, 1), (1, 0)))
+
+        unit = lambda f, *a: lambda n: f(n, *a) if 0 <= n < UNITS else None
+        step = lambda f, *a: lambda s: f(s, *a)
+        stages = {
+            "s00": unit(scores, ((0, 0),)), "s01": unit(scores, ((0, 1),)),
+            "s10": unit(scores, ((1, 0),)), "s11": unit(scores, ((1, 1),)),
+            "m00": unit(mask, ((0, 0),)), "m01": unit(mask, ((0, 1),)),
+            "m10": unit(mask, ((1, 0),)), "m11": unit(mask, ((1, 1),)),
+            "h0": unit(halve, 0), "h1": unit(halve, 1),
+            "n0": unit(negmax, 0), "n1": unit(negmax, 1),
+            "e0": unit(exps, 0), "e1": unit(exps, 1), "rc": unit(recip), "db": unit(double), "dg": unit(diag),
+            "z0": unit(norm, 0), "z1": unit(norm, 1), "a0": unit(turn_p, 0), "a1": unit(turn_p, 1),
+            "g0": unit(gains, 0), "g1": unit(gains, 1), "qp": unit(quant_p), "po": unit(pv), "pp": unit(pvp),
+            "to": unit(take_out), "tp": unit(take_pl), "qo": unit(quant_out),
+            "ta": step(chunk_turn, 0), "tb": step(chunk_turn, 1), "ca": step(chunk_take, 0), "cb": step(chunk_take, 1),
+            "qa": step(chunk_quant, 0), "qb": step(chunk_quant, 1),
+            "xt": step(extra, 0), "xc": step(extra, 1), "xq": step(extra, 2),
+            "ld": step(loads), "bd": make_b, "vg": step(v_group), "vq": step(v_quant),
+        }
+        for s in range(UNITS + 8):
+            for name, lag in BODY:
+                n = s + lag
+                if s == 0 and name in ("s00", "s01", "s10", "ta") and n <= 0:
+                    continue
+                if s == 0 and n < 0:
+                    continue
+                stages[name](n)

from contextlib import ExitStack

import concourse.mybir as mybir
from concourse.masks import make_identity

H, NQ, NK, DK, DV = 2, 1024, 1024, 512, 512
FLOPS = 2 * H * NQ * NK * (2 * DK + DV)

F32 = mybir.dt.float32
BF16 = mybir.dt.bfloat16
U32 = mybir.dt.uint32
I32 = mybir.dt.int32
U8 = mybir.dt.uint8
FP8X4 = mybir.dt.float8_e4m3fn_x4
ALU = mybir.AluOpType
ACT = mybir.ActivationFunctionType

GCONV = ()
PEG = (0,)
GV1 = "s"
BODY = (("po",-4,),("bd",2,),("z0",-2,),("pp",-4,),("m00",0,),("s11",0,),("s10",0,),("ca",0,),("m01",0,),("g0",-3,),("e0",-1,),("ld",0,),("a0",-2,),("to",-4,),("h0",0,),("tb",0,),("vq",0,),("qa",-1,),("m11",0,),("g1",-3,),("m10",0,),("rc",-1,),("h1",0,),("xc",-2,),("qb",-1,),("qo",-5,),("a1",-2,),("vg",0,),("db",-1,),("qp",-3,),("tp",-4,),("s01",1,),("cb",0,),("n1",0,),("xq",-3,),("n0",0,),("s00",1,),("z1",-1,),("dg",-1,),("e1",0,),("ta",1,),("xt",0,),)

P = 128
SCALE = 1.0 / 512.0 ** 0.5
MASKED = -10000.0
EPS = 2.0 ** -14
BOUND = -MASKED / SCALE / EPS
TILES = NQ // P
UNITS = H * TILES


def tile_sanrealfakeedgedualattention_x1_kernel(
    tc, q_real, k_real, q_fake, k_fake, v, adj, key_gain, out_0, out_1, out_2
):
    nc = tc.nc
    queries = (q_real, q_fake)
    keys = (k_real, k_fake)
    words_out = out_1[0].rearrange("p m t -> p (m t)").bitcast(I32)
    scales_out = out_2[0].bitcast(I32)

    with ExitStack() as ctx:
        const = ctx.enter_context(tc.tile_pool(name="const", bufs=1))
        pool = ctx.enter_context(tc.tile_pool(name="work", bufs=2))
        psum = ctx.enter_context(tc.psum_pool(name="psum", bufs=1))
        ctx.enter_context(tc.manual_schedule())

        BANKS = {"s": 3, "y": 2, "o": 2, "t": 1}

        def bank(tag):
            b = psum.tile([P, 512], F32, name=tag, tag=tag, bufs=BANKS[tag])
            return b

        ident = const.tile([P, P], F32, name="ident")
        make_identity(nc, ident[:])

        raws, groups, codes, scales = {}, {}, {}, {}

        def load_chunk(c, t0=0, t1=4):
            kind, br, h, half = c
            if c not in raws:
                raws[c] = pool.tile([P, 4, DK], BF16, name="raw", tag="raw", bufs=10)
            src = (queries if kind == "q" else keys)[br][h, 512 * half : 512 * half + 512, :]
            view = "(t m) k -> m t k" if kind == "q" else "(m t) k -> m t k"
            nc.sync.dma_start(out=raws[c][:, t0:t1, :], in_=src.rearrange(view, t=4)[:, t0:t1, :])

        def turn_chunk(c, part, tag):
            words = raws[c][:].rearrange("p t k -> p (t k)").bitcast(F32)
            b = bank(tag)
            for tt in range(2):
                for u in range(2):
                    w0 = 256 * (2 * part + tt)
                    nc.tensor.transpose(
                        b[:, 128 * (2 * tt + u) : 128 * (2 * tt + u) + 128],
                        words[:, w0 + u : w0 + 256 : 2],
                        ident[:],
                    )
            return b

        def take_chunk(c, part, b, engine):
            grp = pool.tile([P, 256, 4], BF16, name="grp", tag="grp", bufs=6, align_bytes=64)
            groups[c, part] = grp
            dst = grp[:].rearrange("p n j -> p (n j)").bitcast(F32).rearrange("p (s m u) -> p s m u", s=2, u=2)
            src = b[:].rearrange("p (s u m) -> p s m u", s=2, u=2)
            if engine == "v":
                nc.vector.tensor_copy(out=dst, in_=src)
            else:
                nc.scalar.copy(out=dst, in_=src)

        def quant_chunk(c, part):
            kind, br, h, half = c
            key = (kind, br, h)
            if key not in codes:
                codes[key] = pool.tile([P, 1024], U32, name="c" + kind + str(br), bufs=2, align_bytes=64)
                scales[key] = pool.tile([P, 1024], U8, name="s" + kind + str(br), bufs=2, align_bytes=64)
            c0 = 512 * half + 256 * part
            nc.vector.quantize_mx(
                out=codes[key][:, c0 : c0 + 256].bitcast(FP8X4),
                scales=scales[key][:, c0 : c0 + 256],
                in_=groups[c, part][:].rearrange("p n j -> p (n j)"),
            )

        vraw, vcodes, vscales, vgrp = {}, {}, {}, {}

        def load_v(h, g):
            r = pool.tile([P, 4, DV], BF16, name="vraw", tag="raw", bufs=10)
            nc.sync.dma_start(out=r[:], in_=v[h, 512 * g : 512 * g + 512, :].rearrange("(p j) c -> p j c", j=4))
            vraw[h, g] = r

        def group_v(h, g, engine):
            t = pool.tile([P, 512 * 4], BF16, name="vgrp", tag="vgrp", bufs=2, align_bytes=64)
            dst = t[:].rearrange("p (t m j) -> p t m j", t=4, j=4)
            src = vraw[h, g][:].rearrange("p j (m t) -> p t m j", t=4)
            if engine == "s":
                nc.scalar.copy(out=dst, in_=src)
            else:
                nc.vector.tensor_copy(out=dst, in_=src)
            vgrp[h, g] = t

        def quant_v(h, g):
            if g == 0:
                vcodes[h] = const.tile([P, 2, DV], U32, name="vc" + str(h), align_bytes=64)
                vscales[h] = const.tile([P, 2, DV], U8, name="vs" + str(h), align_bytes=64)
            nc.vector.quantize_mx(
                out=vcodes[h][:, g, :].bitcast(FP8X4), scales=vscales[h][:, g, :], in_=vgrp[h, g][:]
            )

        adjs, bounds = {}, {}

        def load_adj(i):
            a = const.tile([P, NK], BF16, name="adj" + str(i))
            nc.sync.dma_start(out=a[:], in_=adj[P * i : P * i + P, :])
            adjs[i] = a

        def make_bounds(i):
            for br, op in enumerate((ALU.is_gt, ALU.is_le)):
                b = const.tile([P, NK], BF16, name="bound" + str(br) + str(i))
                nc.vector.tensor_scalar(
                    out=b[:], in0=adjs[i][:], scalar1=0.0, scalar2=EPS, op0=op, op1=ALU.subtract
                )
                bounds[br, i] = b

        gain_raw = const.tile([P, H, 16], BF16, name="gain_raw")
        gain = const.tile([P, H, 2, 4], F32, name="gain")

        def load_gain():
            for h in range(H):
                nc.sync.dma_start(
                    out=gain_raw[:, h, 0:8].rearrange("p (g t) -> p g t", g=2),
                    in_=key_gain[h].rearrange("(g p t) -> p g t", g=2, t=4),
                )

        def scale_gain():
            nc.vector.tensor_scalar(
                out=gain[:], in0=gain_raw[:, :, 0:8].rearrange("p h (g t) -> p h g t", g=2),
                scalar1=1.0 / 3.0, scalar2=None, op0=ALU.mult,
            )

        sbank, xs, nms, halves, es, zs, rs, diags, ybank, pgs, pcodes, pscales = ({} for _ in range(12))
        obank, wbank, pls, plw, plsc = ({} for _ in range(5))

        def scores(n, parts):
            h, i = divmod(n, TILES)
            for br, g in parts:
                b = bank("s")
                nc.tensor.matmul_mx(
                    out=b[:],
                    lhsT=codes["q", br, h][:, P * i : P * i + P].bitcast(FP8X4),
                    lhsT_scale=scales["q", br, h][:, P * i : P * i + P],
                    rhs=codes["k", br, h][:, 512 * g : 512 * g + 512].bitcast(FP8X4),
                    rhs_scale=scales["k", br, h][:, 512 * g : 512 * g + 512],
                    start=True, stop=True,
                )
                sbank[n, br, g] = b

        def mask(n, parts):
            i = n % TILES
            if n not in xs:
                xs[n] = pool.tile([P, 2, NK], F32, name="x", tag="x", bufs=2)
            for br, g in parts:
                cols = slice(512 * g, 512 * g + 512)
                nc.vector.scalar_tensor_tensor(
                    out=xs[n][:, br, cols].rearrange("p (t m) -> p t m", t=4),
                    in0=bounds[br, i][:, cols].rearrange("p (m t) -> p t m", t=4), scalar=BOUND,
                    in1=sbank[n, br, g][:].rearrange("p (t m) -> p t m", t=4), op0=ALU.mult, op1=ALU.min,
                )

        def halve(n, br):
            if n not in nms:
                nms[n] = pool.tile([P, 2], F32, name="m", tag="m", bufs=3)
            if br in GCONV:
                halves[n, br] = pool.tile([P, NK], BF16, name="neg" + str(br), bufs=2)
                nc.gpsimd.tensor_scalar(
                    out=halves[n, br][:], in0=xs[n][:, br, :], scalar1=-SCALE, scalar2=0.0,
                    op0=ALU.mult, op1=ALU.add,
                )
            else:
                halves[n, br] = pool.tile([P, 512], BF16, name="half" + str(br), bufs=2)
                nc.vector.tensor_tensor(
                    out=halves[n, br][:], in0=xs[n][:, br, 0:512], in1=xs[n][:, br, 512:1024], op=ALU.max
                )

        def negmax(n, br):
            nc.vector.tensor_scalar(
                out=halves[n, br][:], in0=halves[n, br][:], scalar1=1.0 if br in GCONV else -SCALE, scalar2=None,
                op0=ALU.mult, op1=ALU.min, accum_out=nms[n][:, br : br + 1],
            )

        def exps(n, br):
            if n not in es:
                es[n] = pool.tile([P, 2, NK], F32, name="e", tag="e", bufs=2)
                zs[n] = pool.tile([P, 2], F32, name="z", tag="z", bufs=3)
            nc.scalar.activation(
                out=es[n][:, br, :], in_=xs[n][:, br, :], func=ACT.Exp,
                bias=nms[n][:, br : br + 1], scale=SCALE, accum_out=zs[n][:, br : br + 1],
            )

        def pe_norm(n, g):
            return n < UNITS - 2 and g in PEG

        def double(n):
            nc.vector.tensor_scalar(
                out=rs[n][:, 0:1], in0=rs[n][:, 0:1], scalar1=2.0, scalar2=None, op0=ALU.mult
            )

        def recip(n):
            rs[n] = pool.tile([P, 2], F32, name="r", tag="r", bufs=3)
            nc.vector.reciprocal(out=rs[n][:], in_=zs[n][:])

        def diag(n):
            if pe_norm(n, 0):
                diags[n] = pool.tile([P, P], F32, name="diag", tag="diag", bufs=3)
                nc.gpsimd.tensor_scalar(
                    out=diags[n][:], in0=ident[:], scalar1=rs[n][:, 0:1], scalar2=0.0, op0=ALU.mult, op1=ALU.add
                )

        def norm(n, br):
            cut = 512 if pe_norm(n, 0) else 0
            real = es[n][:, 0, cut:NK]
            fake = es[n][:, 1, :]
            if br and n == UNITS - 1:
                nc.vector.tensor_scalar(
                    out=fake[:, 512:NK], in0=fake[:, 512:NK], scalar1=rs[n][:, 1:2], scalar2=None, op0=ALU.mult
                )
                nc.scalar.activation(out=fake[:, 0:512], in_=fake[:, 0:512], func=ACT.Copy, scale=rs[n][:, 1:2])
            elif br:
                nc.scalar.activation(out=fake, in_=fake, func=ACT.Copy, scale=rs[n][:, 1:2])
            elif n >= UNITS - 2:
                nc.vector.tensor_scalar(
                    out=real, in0=real, scalar1=rs[n][:, 0:1], scalar2=None, op0=ALU.mult
                )
            else:
                nc.scalar.activation(out=real, in_=real, func=ACT.Copy, scale=rs[n][:, 0:1])

        def turn_p(n, g):
            b = bank("y")
            for t in range(4):
                col = 512 * g + 128 * t
                out = b[:, 128 * t : 128 * t + 128]
                for k, br in enumerate((t % 2, 1 - t % 2)):
                    by_diag = br == 0 and pe_norm(n, g)
                    nc.tensor.matmul(
                        out, lhsT=es[n][:, br, col : col + 128], rhs=(diags[n] if by_diag else ident)[:],
                        start=(k == 0), stop=(k == 1), is_transpose=not by_diag,
                    )
            ybank[n, g] = b

        def gains(n, g):
            if n not in pgs:
                pgs[n] = pool.tile([P, 2, P, 4], BF16, name="pg", tag="pg", bufs=2, align_bytes=64)
            nc.vector.tensor_tensor(
                out=pgs[n][:, g],
                in0=ybank[n, g][:].rearrange("p (t m) -> p m t", t=4),
                in1=gain[:, n // TILES, g, :].unsqueeze(1).to_broadcast([P, P, 4]),
                op=ALU.mult,
            )

        def quant_p(n):
            pcodes[n] = pool.tile([P, 2, P], U32, name="pc", tag="pc", bufs=2, align_bytes=64)
            pscales[n] = pool.tile([P, 2, P], U8, name="ps", tag="ps", bufs=2, align_bytes=64)
            nc.vector.quantize_mx(
                out=pcodes[n][:].rearrange("p g m -> p (g m)").bitcast(FP8X4),
                scales=pscales[n][:].rearrange("p g m -> p (g m)"),
                in_=pgs[n][:].rearrange("p g m t -> p (g m t)"),
            )

        def pv(n):
            h = n // TILES
            obank[n] = bank("o")
            for g in range(2):
                nc.tensor.matmul_mx(
                    out=obank[n][:],
                    lhsT=pcodes[n][:, g, :].bitcast(FP8X4), lhsT_scale=pscales[n][:, g, :],
                    rhs=vcodes[h][:, g, :].bitcast(FP8X4), rhs_scale=vscales[h][:, g, :],
                    start=(g == 0), stop=(g == 1),
                )

        def pvp(n):
            h = n // TILES
            wbank[n] = bank("o")
            for t in range(4):
                cols = slice(128 * t, 128 * t + 128)
                for g in range(2):
                    nc.tensor.matmul_mx(
                        out=wbank[n][:, cols],
                        lhsT=vcodes[h][:, g, cols].bitcast(FP8X4), lhsT_scale=vscales[h][:, g, cols],
                        rhs=pcodes[n][:, g, :].bitcast(FP8X4), rhs_scale=pscales[n][:, g, :],
                        start=(g == 0), stop=(g == 1),
                    )

        def take_out(n):
            h, i = divmod(n, TILES)
            o = pool.tile([P, DV], F32, name="o_sb", tag="o_sb", bufs=2)
            nc.scalar.copy(
                out=o[:].rearrange("p (m t) -> p m t", t=4),
                in_=obank[n][:].rearrange("p (t m) -> p m t", t=4),
            )
            nc.sync.dma_start(out=out_0[h, P * i : P * i + P, :], in_=o[:])

        def take_pl(n):
            pls[n] = pool.tile([P, P, 4], BF16, name="pl", tag="pl", bufs=3, align_bytes=64)
            copy = nc.vector.tensor_copy if n >= UNITS - 2 else nc.scalar.copy
            copy(out=pls[n][:], in_=wbank[n][:].rearrange("p (t m) -> p m t", t=4))

        def quant_out(n):
            h, i = divmod(n, TILES)
            if i == 0:
                plw[h] = const.tile([P, NQ], U32, name="plw" + str(h), align_bytes=64)
                plsc[h] = const.tile([P, NQ], U8, name="plsc" + str(h), align_bytes=64)
            cols = slice(P * i, P * i + P)
            nc.vector.quantize_mx(
                out=plw[h][:, cols].bitcast(FP8X4), scales=plsc[h][:, cols],
                in_=pls[n][:].rearrange("p m t -> p (m t)"),
            )
            done = {3: (0, 4), 6: (4, 7), 7: (7, 8)}.get(i)
            if done:
                c0, c1 = P * done[0], P * done[1]
                nc.sync.dma_start(
                    out=words_out[:, NQ * h + c0 : NQ * h + c1], in_=plw[h][:, c0:c1].bitcast(I32)
                )
            if i == TILES - 1:
                for big in range(4):
                    nc.sync.dma_start(
                        out=scales_out[4 * big : 4 * big + 4, NQ // 4 * h : NQ // 4 * (h + 1)],
                        in_=plsc[h][32 * big : 32 * big + 4, :].bitcast(I32),
                    )

        def both(half, h, part):
            return [(("q", 0, h, half), part), (("q", 1, h, half), part)]

        def whole(br, half):
            return [(("k", br, 1, half), 0), (("k", br, 1, half), 1)]

        prep = {
            0: both(0, 0, 1) + whole(0, 0), 1: whole(0, 1), 2: both(1, 0, 0), 3: whole(1, 0), 4: both(1, 0, 1),
            5: whole(1, 1), 6: both(0, 1, 0), 7: both(0, 1, 1), 9: both(1, 1, 0), 11: both(1, 1, 1),
        }

        def later(s):
            return prep.get(s, [])

        load_chunk(("q", 0, 0, 0), 0, 2)
        load_chunk(("k", 0, 0, 0))
        load_adj(0)
        load_chunk(("k", 0, 0, 1))
        load_chunk(("q", 1, 0, 0), 0, 2)
        load_chunk(("k", 1, 0, 0))
        load_adj(1)
        load_chunk(("k", 1, 0, 1))
        load_adj(2)
        load_v(0, 0)
        load_chunk(("q", 0, 0, 0), 2, 4)
        load_chunk(("q", 1, 0, 0), 2, 4)
        load_gain()
        load_chunk(("k", 0, 1, 0))
        load_adj(3)
        load_v(0, 1)
        load_chunk(("k", 0, 1, 1))
        load_chunk(("q", 0, 0, 1))
        load_chunk(("q", 1, 0, 1))
        for i in range(4, TILES):
            load_adj(i)

        first = [(("q", 0, 0, 0), 0), (("k", 0, 0, 0), 0), (("k", 0, 0, 0), 1), (("k", 0, 0, 1), 0), (("k", 0, 0, 1), 1),
                 (("q", 1, 0, 0), 0), (("k", 1, 0, 0), 0), (("k", 1, 0, 0), 1), (("k", 1, 0, 1), 0), (("k", 1, 0, 1), 1)]
        rotation = "sssyyootyo"
        for k, (c, part) in enumerate(first):
            take_chunk(c, part, turn_chunk(c, part, rotation[k]), "ssssssssss"[k])
            if k in (1, 7, 9):
                make_bounds((1, 7, 9).index(k))
            quant_chunk(c, part)
        scores(0, ((0, 0), (0, 1), (1, 0)))
        turned0 = turn_chunk(*later(0)[0], "t")
        group_v(0, 0, "s")

        first_step = {"ta": -1}
        turned = {(0, 0): turned0}

        def chunk_turn(s, k):
            if s in prep:
                turned[s, k] = turn_chunk(*prep[s][k], "t")

        def chunk_take(s, k):
            if s in prep:
                take_chunk(*prep[s][k], turned[s, k], "s")

        def chunk_quant(s, k):
            if s in prep:
                quant_chunk(*prep[s][k])

        def extra(s, what):
            if s == 0:
                for k, item in enumerate(prep[0][2:]):
                    if what == 0:
                        turned[0, 2 + k] = turn_chunk(*item, "o")
                    elif what == 1:
                        take_chunk(*item, turned[0, 2 + k], "s")
                    else:
                        quant_chunk(*item)

        def loads(s):
            if s >= 0:
                for c, part in later(s + 2):
                    if c not in raws:
                        load_chunk(c)
                if s in (3, 4):
                    load_v(1, s - 3)

        def make_b(i):
            if 3 <= i < TILES:
                make_bounds(i)

        def v_group(s):
            if s == 1:
                group_v(0, 1, "s")
            if s in (7, 8):
                group_v(1, s - 7, GV1)

        def v_quant(s):
            if s == 0:
                scale_gain()
            if s in (1, 2):
                quant_v(0, s - 1)
            if s in (8, 9):
                quant_v(1, s - 8)

        unit = lambda f, *a: lambda n: f(n, *a) if 0 <= n < UNITS else None
        step = lambda f, *a: lambda s: f(s, *a)
        stages = {
            "s00": unit(scores, ((0, 0),)), "s01": unit(scores, ((0, 1),)),
            "s10": unit(scores, ((1, 0),)), "s11": unit(scores, ((1, 1),)),
            "m00": unit(mask, ((0, 0),)), "m01": unit(mask, ((0, 1),)),
            "m10": unit(mask, ((1, 0),)), "m11": unit(mask, ((1, 1),)),
            "h0": unit(halve, 0), "h1": unit(halve, 1),
            "n0": unit(negmax, 0), "n1": unit(negmax, 1),
            "e0": unit(exps, 0), "e1": unit(exps, 1), "rc": unit(recip), "db": unit(double), "dg": unit(diag),
            "z0": unit(norm, 0), "z1": unit(norm, 1), "a0": unit(turn_p, 0), "a1": unit(turn_p, 1),
            "g0": unit(gains, 0), "g1": unit(gains, 1), "qp": unit(quant_p), "po": unit(pv), "pp": unit(pvp),
            "to": unit(take_out), "tp": unit(take_pl), "qo": unit(quant_out),
            "ta": step(chunk_turn, 0), "tb": step(chunk_turn, 1), "ca": step(chunk_take, 0), "cb": step(chunk_take, 1),
            "qa": step(chunk_quant, 0), "qb": step(chunk_quant, 1),
            "xt": step(extra, 0), "xc": step(extra, 1), "xq": step(extra, 2),
            "ld": step(loads), "bd": make_b, "vg": step(v_group), "vq": step(v_quant),
        }
        for s in range(UNITS + 8):
            for name, lag in BODY:
                n = s + lag
                if s == 0 and name in ("s00", "s01", "s10", "ta") and n <= 0:
                    continue
                if s == 0 and n < 0:
                    continue
                stages[name](n)
